import numpy as np
import ml_dtypes


def mxq(x, axis, fmt="e4m3"):
    dtype, down = {"e4m3": (ml_dtypes.float8_e4m3fn, 7), "e5m2": (ml_dtypes.float8_e5m2, 14)}[fmt]
    v = np.moveaxis(np.asarray(x, np.float32).astype(ml_dtypes.bfloat16).astype(np.float64), axis, -1)
    blocks = v.reshape(v.shape[:-1] + (-1, 32))
    amax = np.abs(blocks).max(-1, keepdims=True)
    byte = np.maximum(np.where(amax > 0, np.frexp(amax)[1] - 1 + 127, 0) - down, 1)
    scale = np.exp2(byte - 127.0)
    codes = (blocks / scale).astype(np.float32).astype(dtype).astype(np.float64)
    return np.moveaxis((codes * scale).reshape(v.shape), -1, axis)


WIDE = False


def mx_kscale(k):
    if not WIDE:
        return np.ones(k)
    levels = np.array([10, -10, 5, -5, 0])
    if k % 512:
        return np.exp2(np.random.permutation(np.resize(levels, k // 32))).repeat(32)
    a = np.empty((k // 512, 16))
    for p in range(k // 512):
        a[p, :8] = np.random.permutation(np.resize(levels, 8))
        for g in range(8):
            far = levels[np.abs(levels - a[p, g]) >= 10]
            a[p, g + 8] = far[np.random.randint(len(far))]
    return np.exp2(a.ravel()).repeat(32)


def f64(x):
    return np.asarray(x).astype(np.float64)


def striped(idx):
    return np.tile(idx.reshape(-1, 16).T, (8, 1)).astype(np.uint16)


def unstriped(offs):
    return offs[:16].T.reshape(-1).astype(np.int64)


def pack_weight(w):
    k, n = w.shape
    w = f64(np.asarray(w, np.float32).astype(ml_dtypes.bfloat16)).reshape(k // 32, 32, n)
    amax = np.abs(w).max(1)
    byte = np.clip(np.where(amax > 0, np.frexp(amax)[1] - 1 + 127 - 7, 1), 1, 254)
    scaled = (w * np.exp2(127.0 - byte)[:, None, :]).reshape(k, n).astype(np.float32)
    words = np.ascontiguousarray(scaled.reshape(k // 512, 128, 4, n).transpose(0, 1, 3, 2)).astype(ml_dtypes.float8_e4m3fn).view(np.uint8)
    return words, np.ascontiguousarray(byte.astype(np.uint8).reshape(k // 512, 16, n))


def unpack_weight(words, scales):
    g, p, n, _ = words.shape
    vals = np.ascontiguousarray(words).view(ml_dtypes.float8_e4m3fn).astype(np.float64) * np.repeat(np.exp2(scales.astype(np.float64) - 127.0), 8, axis=1)[..., None]
    return vals.transpose(0, 1, 3, 2).reshape(g * 512, n)


K, T, E, C, N = 1536, 1024, 2, 256, 256


def by_expert(wq, xq):
    return np.concatenate([wq[e].T @ xq[:, e * C:(e + 1) * C] for e in range(E)], axis=1)


def setup_inputs():
    n = np.random.standard_normal
    s = mx_kscale(K)[:, None]
    packed = [pack_weight(m) for m in n((E, K, N)) / np.sqrt(K) / s[None]]
    return {
        "xT": (n((K, T)) * s).astype(np.float32),
        "w_words": np.stack([m[0] for m in packed]),
        "w_scales": np.stack([m[1] for m in packed]),
        "gate": np.tile(np.random.uniform(0.2, 1.0, E * C), (N, 1)).astype(np.float32),
        "offs": striped(np.random.permutation(T)[:E * C]),
    }


def reference(xT, w_words, w_scales, gate, offs):
    idx = unstriped(offs)
    xq = mxq(f64(xT)[:, idx], 0, "e4m3")
    w = np.stack([unpack_weight(w_words[e], w_scales[e]) for e in range(E)])
    y = by_expert(w, xq)
    out = np.zeros((N, T))
    out[:, idx] = f64(gate) * y
    return out

@@ -1,0 +1,135 @@
+from contextlib import ExitStack
+
+import concourse.mybir as mybir
+
+K, T, E, C, N = 1536, 1024, 2, 256, 256
+S = E * C
+P = 128
+PASSES = K // 512
+BLOCKS = N // P
+
+FLOPS = 2 * S * K * N
+BYTES = 4 * K * T + E * K * N + E * K * N // 32 + 4 * S + 2 * 8 * 16 * (S // 16) + 4 * N * T
+
+F32 = mybir.dt.float32
+BF16 = mybir.dt.bfloat16
+I32 = mybir.dt.int32
+U32 = mybir.dt.uint32
+U16 = mybir.dt.uint16
+U8 = mybir.dt.uint8
+FP8X4 = mybir.dt.float8_e4m3fn_x4
+MULT = mybir.AluOpType.mult
+
+LOADS = [[(0, 1024)], [(0, 1024)], [(0, 512), (512, 256), (768, 256)]]
+CASTS = [[(0, 512, 288), (512, 512, 352)], [(0, 512, 384), (512, 512, 224)], [(0, 512, 192), (512, 256, 32), (768, 256, 128)]]
+
+
+def tile_routed_moe_kernel(tc, xT, w_words, w_scales, gate, offs, out):
+    nc = tc.nc
+    with ExitStack() as ctx:
+        keep = ctx.enter_context(tc.tile_pool(name="keep", bufs=1))
+        ring = ctx.enter_context(tc.tile_pool(name="ring", bufs=3))
+        psum = ctx.enter_context(tc.psum_pool(name="psum", bufs=1))
+
+        warm = keep.tile([P, 16], F32, name="warm")
+        warm_out = keep.tile([P, 16], BF16, name="warm_out")
+        nc.vector.memset(warm[:], 0.0)
+        nc.scalar.copy(out=warm_out[:], in_=warm[:])
+
+        planes = keep.tile([P, T], U8, name="planes", align_bytes=64)
+        nc.gpsimd.memset(planes[:], 0)
+        w_planes = keep.tile([P, E * PASSES, N], U8, name="w_planes", align_bytes=64)
+        nc.vector.memset(w_planes[:].rearrange("p a n -> p (a n)").bitcast(I32), 0)
+        windows = []
+        for b in range(BLOCKS):
+            window = keep.tile([P, T], F32, name=f"window{b}")
+            nc.vector.memset(window[:], 0.0)
+            windows.append(window)
+
+        x_rows = xT.rearrange("(g p r) t -> g p r t", p=P, r=4)
+        raws = []
+        offsets = keep.tile([P, S // 16], U16, name="offsets")
+        for g in range(PASSES):
+            for t0, n in LOADS[g]:
+                raw = keep.tile([P, 4, n], F32, name=f"raw{g}_{t0}")
+                nc.sync.dma_start(raw[:], x_rows[g, :, :, t0 : t0 + n])
+                raws.append((g, t0, n, raw))
+            if g == 0:
+                nc.sync.dma_start(offsets[:], offs)
+
+        w_codes = keep.tile([P, E, PASSES, N], U32, name="w_codes", align_bytes=64)
+        for q in range(4):
+            nc.sync.dma_start(
+                w_planes[32 * q : 32 * q + 4, :, :].bitcast(I32),
+                w_scales[:, :, 4 * q : 4 * q + 4, :].rearrange("e a q n -> q (e a) n").bitcast(I32),
+            )
+        for e in range(E):
+            nc.sync.dma_start(
+                w_codes[:, e, :, :].bitcast(I32),
+                w_words[e].rearrange("a p n r -> p a (n r)").bitcast(I32),
+            )
+        gates = keep.tile([P, S], F32, name="gates")
+        nc.sync.dma_start(gates[:], gate[0:P, :])
+
+        x_codes = keep.tile([P, PASSES, S], U32, name="x_codes", align_bytes=64)
+        x_planes = keep.tile([P, S], U8, name="x_planes", align_bytes=64)
+        sums = {}
+        for e in range(E):
+            for b in range(BLOCKS):
+                acc = psum.tile([P, C], F32, name=f"acc{e}{b}")
+                sums[e, b] = acc
+
+        for g in range(PASSES):
+            codes = keep.tile([P, T], U32, name=f"codes{g}", align_bytes=64)
+            for t0, n, v in CASTS[g]:
+                grouped = ring.tile([P, n, 4], BF16, name="grouped", align_bytes=64)
+                first, raw = [(l0, tile) for lg, l0, ln, tile in raws if lg == g and l0 <= t0 < l0 + ln][0]
+                o = t0 - first
+                dst = grouped[:].rearrange("p (c i) r -> p c r i", i=4)
+                src = raw[:, :, o : o + n].rearrange("p r (c i) -> p c r i", i=4)
+                c = v // 4
+                if v:
+                    nc.vector.tensor_copy(out=dst[:, :c], in_=src[:, :c])
+                if v < n:
+                    nc.scalar.copy(out=dst[:, c:], in_=src[:, c:])
+                nc.vector.quantize_mx(
+                    out=codes[:, t0 : t0 + n].bitcast(FP8X4),
+                    scales=planes[4 * g : P, t0 : t0 + n],
+                    in_=grouped[:].rearrange("p t r -> p (t r)"),
+                )
+            if g < PASSES - 1:
+                nc.vector.tensor_copy(out=x_codes[:, g, :], in_=codes[:].indirect(offsets[:]))
+            else:
+                for e in range(E):
+                    cols = slice(e * C, (e + 1) * C)
+                    entries = offsets[:, e * C // 16 : (e + 1) * C // 16]
+                    nc.vector.tensor_copy(out=x_planes[:, cols], in_=planes[:].indirect(entries))
+                    nc.vector.tensor_copy(out=x_codes[:, g, cols], in_=codes[:].indirect(entries))
+
+        ys = {}
+        for e in range(E):
+            cols = slice(e * C, (e + 1) * C)
+            for b in range(BLOCKS):
+                rows = slice(b * P, (b + 1) * P)
+                for g in range(PASSES):
+                    nc.tensor.matmul_mx(
+                        out=sums[e, b][:],
+                        lhsT=w_codes[:, e, g, rows].bitcast(FP8X4),
+                        lhsT_scale=w_planes[:, e * PASSES + g, rows],
+                        rhs=x_codes[:, g, cols].bitcast(FP8X4),
+                        rhs_scale=x_planes[4 * g : P, cols],
+                        start=(g == 0),
+                        stop=(g == PASSES - 1),
+                    )
+                y = keep.tile([P, C], F32, name=f"y{e}{b}")
+                nc.scalar.copy(out=y[:], in_=sums[e, b][:])
+                ys[e, b] = y
+        for b in range(BLOCKS):
+            for e in range(E):
+                nc.vector.tensor_tensor(
+                    out=windows[b][:].indirect(offsets[:, e * C // 16 : (e + 1) * C // 16]),
+                    in0=ys[e, b][:],
+                    in1=gates[:, e * C : (e + 1) * C],
+                    op=MULT,
+                )
+            nc.sync.dma_start(out[b * P : (b + 1) * P, :], windows[b][:])

@@ -20,15 +20,14 @@ U8 = mybir.dt.uint8
 FP8X4 = mybir.dt.float8_e4m3fn_x4
 MULT = mybir.AluOpType.mult
 
-LOADS = [[(0, 1024)], [(0, 1024)], [(0, 512), (512, 256), (768, 256)]]
-CASTS = [[(0, 512, 288), (512, 512, 352)], [(0, 512, 384), (512, 512, 224)], [(0, 512, 192), (512, 256, 32), (768, 256, 128)]]
+FIRST = 128
+ON_VECTOR = [704, 512, 448, 384, 384, 512]
 
 
 def tile_routed_moe_kernel(tc, xT, w_words, w_scales, gate, offs, out):
     nc = tc.nc
     with ExitStack() as ctx:
         keep = ctx.enter_context(tc.tile_pool(name="keep", bufs=1))
-        ring = ctx.enter_context(tc.tile_pool(name="ring", bufs=3))
         psum = ctx.enter_context(tc.psum_pool(name="psum", bufs=1))
 
         warm = keep.tile([P, 16], F32, name="warm")
@@ -36,8 +35,6 @@ def tile_routed_moe_kernel(tc, xT, w_words, w_scales, gate, offs, out):
         nc.vector.memset(warm[:], 0.0)
         nc.scalar.copy(out=warm_out[:], in_=warm[:])
 
-        planes = keep.tile([P, T], U8, name="planes", align_bytes=64)
-        nc.gpsimd.memset(planes[:], 0)
         w_planes = keep.tile([P, E * PASSES, N], U8, name="w_planes", align_bytes=64)
         nc.vector.memset(w_planes[:].rearrange("p a n -> p (a n)").bitcast(I32), 0)
         windows = []
@@ -46,16 +43,16 @@ def tile_routed_moe_kernel(tc, xT, w_words, w_scales, gate, offs, out):
             nc.vector.memset(window[:], 0.0)
             windows.append(window)
 
-        x_rows = xT.rearrange("(g p r) t -> g p r t", p=P, r=4)
-        raws = []
+        x_rows = xT.rearrange("(g p u r) t -> g u p r t", p=P, u=2, r=2)
+        raws = {}
         offsets = keep.tile([P, S // 16], U16, name="offsets")
         for g in range(PASSES):
-            for t0, n in LOADS[g]:
-                raw = keep.tile([P, 4, n], F32, name=f"raw{g}_{t0}")
-                nc.sync.dma_start(raw[:], x_rows[g, :, :, t0 : t0 + n])
-                raws.append((g, t0, n, raw))
-            if g == 0:
-                nc.sync.dma_start(offsets[:], offs)
+            for u in range(2):
+                raw = keep.tile([P, 2, T], F32, name=f"raw{g}{u}", tag=f"raw{g}{u}", align_bytes=64)
+                nc.sync.dma_start(raw[:], x_rows[g, u])
+                raws[g, u] = raw
+                if (g, u) == (0, 0):
+                    nc.sync.dma_start(offsets[:], offs)
 
         w_codes = keep.tile([P, E, PASSES, N], U32, name="w_codes", align_bytes=64)
         for q in range(4):
@@ -63,73 +60,90 @@ def tile_routed_moe_kernel(tc, xT, w_words, w_scales, gate, offs, out):
                 w_planes[32 * q : 32 * q + 4, :, :].bitcast(I32),
                 w_scales[:, :, 4 * q : 4 * q + 4, :].rearrange("e a q n -> q (e a) n").bitcast(I32),
             )
+        gates = keep.tile([P, S], F32, name="gates")
         for e in range(E):
             nc.sync.dma_start(
                 w_codes[:, e, :, :].bitcast(I32),
                 w_words[e].rearrange("a p n r -> p a (n r)").bitcast(I32),
             )
-        gates = keep.tile([P, S], F32, name="gates")
-        nc.sync.dma_start(gates[:], gate[0:P, :])
+            if e == 0:
+                nc.sync.dma_start(gates[:], gate[0:P, :])
 
         x_codes = keep.tile([P, PASSES, S], U32, name="x_codes", align_bytes=64)
-        x_planes = keep.tile([P, S], U8, name="x_planes", align_bytes=64)
-        sums = {}
-        for e in range(E):
-            for b in range(BLOCKS):
-                acc = psum.tile([P, C], F32, name=f"acc{e}{b}")
-                sums[e, b] = acc
+        x_planes = keep.tile([P, PASSES, S], U8, name="x_planes", align_bytes=64)
 
+        picked = [keep.tile([P, 2, S], U32, name=f"picked{g}") for g in range(PASSES)]
+        pairs = {}
+        grouped = {}
+
+        def cast(g, u):
+            pairs[g, u] = keep.tile([P, T], U32, name=f"pairs{g}{u}")
+            dst = pairs[g, u][:].bitcast(BF16).rearrange("p (c i r) -> p c r i", i=4, r=2)
+            src = raws[g, u][:].rearrange("p r (c i) -> p c r i", i=4)
+            c = ON_VECTOR[2 * g + u] // 4
+            nc.vector.tensor_copy(out=dst[:, :c], in_=src[:, :c])
+            nc.scalar.copy(out=dst[:, c:], in_=src[:, c:])
+
+        def gather(g, u, s0, s1):
+            nc.vector.tensor_copy(out=picked[g][:, u, s0:s1], in_=pairs[g, u][:].indirect(offsets[:, s0 // 16 : s1 // 16]))
+
+        def interleave(g, s0, s1, tag):
+            grouped[g, s0] = keep.tile([P, 2 * (s1 - s0)], U32, name=f"grouped{g}_{s0}", tag=tag, align_bytes=64)
+            nc.scalar.copy(
+                out=grouped[g, s0][:].rearrange("p (s u) -> p s u", u=2),
+                in_=picked[g][:, :, s0:s1].rearrange("p u s -> p s u"),
+            )
+
+        def quantise(g, s0, s1):
+            nc.vector.quantize_mx(
+                out=x_codes[:, g, s0:s1].bitcast(FP8X4),
+                scales=x_planes[:, g, s0:s1],
+                in_=grouped[g, s0][:].bitcast(BF16),
+            )
+
+        last = PASSES - 1
+        cast(0, 0)
         for g in range(PASSES):
-            codes = keep.tile([P, T], U32, name=f"codes{g}", align_bytes=64)
-            for t0, n, v in CASTS[g]:
-                grouped = ring.tile([P, n, 4], BF16, name="grouped", align_bytes=64)
-                first, raw = [(l0, tile) for lg, l0, ln, tile in raws if lg == g and l0 <= t0 < l0 + ln][0]
-                o = t0 - first
-                dst = grouped[:].rearrange("p (c i) r -> p c r i", i=4)
-                src = raw[:, :, o : o + n].rearrange("p r (c i) -> p c r i", i=4)
-                c = v // 4
-                if v:
-                    nc.vector.tensor_copy(out=dst[:, :c], in_=src[:, :c])
-                if v < n:
-                    nc.scalar.copy(out=dst[:, c:], in_=src[:, c:])
-                nc.vector.quantize_mx(
-                    out=codes[:, t0 : t0 + n].bitcast(FP8X4),
-                    scales=planes[4 * g : P, t0 : t0 + n],
-                    in_=grouped[:].rearrange("p t r -> p (t r)"),
-                )
-            if g < PASSES - 1:
-                nc.vector.tensor_copy(out=x_codes[:, g, :], in_=codes[:].indirect(offsets[:]))
-            else:
-                for e in range(E):
-                    cols = slice(e * C, (e + 1) * C)
-                    entries = offsets[:, e * C // 16 : (e + 1) * C // 16]
-                    nc.vector.tensor_copy(out=x_planes[:, cols], in_=planes[:].indirect(entries))
-                    nc.vector.tensor_copy(out=x_codes[:, g, cols], in_=codes[:].indirect(entries))
+            gather(g, 0, 0, S)
+            if g > 0:
+                quantise(g - 1, 0, S)
+            cast(g, 1)
+            if g < last:
+                gather(g, 1, 0, S)
+                cast(g + 1, 0)
+                interleave(g, 0, S, f"raw{g + 1}0")
+        cuts = [(0, FIRST), (FIRST, C), (C, S)]
+        for s0, s1 in cuts:
+            gather(last, 1, s0, s1)
+        for s0, s1 in cuts:
+            interleave(last, s0, s1, f"grouped{s0}")
+            quantise(last, s0, s1)
 
-        ys = {}
-        for e in range(E):
-            cols = slice(e * C, (e + 1) * C)
-            for b in range(BLOCKS):
-                rows = slice(b * P, (b + 1) * P)
+        units = [(b, s0, s1) for s0, s1 in cuts for b in range(BLOCKS)]
+        for b, s0, s1 in units:
+            rows = slice(b * P, (b + 1) * P)
+            acc = psum.tile([P, s1 - s0], F32, name=f"acc{b}_{s0}")
+            for e in range(E):
+                c0, c1 = max(s0, e * C), min(s1, (e + 1) * C)
+                if c0 >= c1:
+                    continue
                 for g in range(PASSES):
                     nc.tensor.matmul_mx(
-                        out=sums[e, b][:],
+                        out=acc[:, c0 - s0 : c1 - s0],
                         lhsT=w_codes[:, e, g, rows].bitcast(FP8X4),
                         lhsT_scale=w_planes[:, e * PASSES + g, rows],
-                        rhs=x_codes[:, g, cols].bitcast(FP8X4),
-                        rhs_scale=x_planes[4 * g : P, cols],
+                        rhs=x_codes[:, g, c0:c1].bitcast(FP8X4),
+                        rhs_scale=x_planes[:, g, c0:c1],
                         start=(g == 0),
                         stop=(g == PASSES - 1),
                     )
-                y = keep.tile([P, C], F32, name=f"y{e}{b}")
-                nc.scalar.copy(out=y[:], in_=sums[e, b][:])
-                ys[e, b] = y
-        for b in range(BLOCKS):
-            for e in range(E):
-                nc.vector.tensor_tensor(
-                    out=windows[b][:].indirect(offsets[:, e * C // 16 : (e + 1) * C // 16]),
-                    in0=ys[e, b][:],
-                    in1=gates[:, e * C : (e + 1) * C],
-                    op=MULT,
-                )
-            nc.sync.dma_start(out[b * P : (b + 1) * P, :], windows[b][:])
+            y = keep.tile([P, s1 - s0], F32, name=f"y{b}_{s0}")
+            nc.scalar.copy(out=y[:], in_=acc[:])
+            nc.vector.tensor_tensor(
+                out=windows[b][:].indirect(offsets[:, s0 // 16 : s1 // 16]),
+                in0=y[:],
+                in1=gates[:, s0:s1],
+                op=MULT,
+            )
+            if s1 == S:
+                nc.sync.dma_start(out[b * P : (b + 1) * P, :], windows[b][:])

@@ -6,6 +6,7 @@ K, T, E, C, N = 1536, 1024, 2, 256, 256
 S = E * C
 P = 128
 PASSES = K // 512
+LAST = PASSES - 1
 BLOCKS = N // P
 
 FLOPS = 2 * S * K * N
@@ -20,8 +21,9 @@ U8 = mybir.dt.uint8
 FP8X4 = mybir.dt.float8_e4m3fn_x4
 MULT = mybir.AluOpType.mult
 
-FIRST = 128
-ON_VECTOR = [704, 512, 448, 384, 384, 512]
+CUTS = [(0, C // 2), (C // 2, C), (C, S)]
+ON_VECTOR = [672, 600, 600, 480, 520, 560]
+RUN = 4
 
 
 def tile_routed_moe_kernel(tc, xT, w_words, w_scales, gate, offs, out):
@@ -29,11 +31,6 @@ def tile_routed_moe_kernel(tc, xT, w_words, w_scales, gate, offs, out):
     with ExitStack() as ctx:
         keep = ctx.enter_context(tc.tile_pool(name="keep", bufs=1))
         psum = ctx.enter_context(tc.psum_pool(name="psum", bufs=1))
-
-        warm = keep.tile([P, 16], F32, name="warm")
-        warm_out = keep.tile([P, 16], BF16, name="warm_out")
-        nc.vector.memset(warm[:], 0.0)
-        nc.scalar.copy(out=warm_out[:], in_=warm[:])
 
         w_planes = keep.tile([P, E * PASSES, N], U8, name="w_planes", align_bytes=64)
         nc.vector.memset(w_planes[:].rearrange("p a n -> p (a n)").bitcast(I32), 0)
@@ -71,79 +68,78 @@ def tile_routed_moe_kernel(tc, xT, w_words, w_scales, gate, offs, out):
 
         x_codes = keep.tile([P, PASSES, S], U32, name="x_codes", align_bytes=64)
         x_planes = keep.tile([P, PASSES, S], U8, name="x_planes", align_bytes=64)
-
-        picked = [keep.tile([P, 2, S], U32, name=f"picked{g}") for g in range(PASSES)]
+        picked = [keep.tile([P, 2, S], U32, name=f"picked{g}", align_bytes=64) for g in range(PASSES)]
         pairs = {}
-        grouped = {}
+
+        def entries(s0, s1):
+            return offsets[:, s0 // 16 : s1 // 16]
 
         def cast(g, u):
-            pairs[g, u] = keep.tile([P, T], U32, name=f"pairs{g}{u}")
-            dst = pairs[g, u][:].bitcast(BF16).rearrange("p (c i r) -> p c r i", i=4, r=2)
-            src = raws[g, u][:].rearrange("p r (c i) -> p c r i", i=4)
-            c = ON_VECTOR[2 * g + u] // 4
-            nc.vector.tensor_copy(out=dst[:, :c], in_=src[:, :c])
-            nc.scalar.copy(out=dst[:, c:], in_=src[:, c:])
+            pairs[g, u] = keep.tile([P, T], U32, name=f"pairs{g}{u}", align_bytes=64)
+            dst = pairs[g, u][:].bitcast(BF16).rearrange("p (c i r) -> p c r i", i=RUN, r=2)
+            src = raws[g, u][:].rearrange("p r (c i) -> p c r i", i=RUN)
+            runs = ON_VECTOR[2 * g + u] // RUN
+            nc.vector.tensor_copy(out=dst[:, :runs], in_=src[:, :runs])
+            nc.scalar.copy(out=dst[:, runs:], in_=src[:, runs:])
 
         def gather(g, u, s0, s1):
-            nc.vector.tensor_copy(out=picked[g][:, u, s0:s1], in_=pairs[g, u][:].indirect(offsets[:, s0 // 16 : s1 // 16]))
+            nc.vector.tensor_copy(out=picked[g][:, u, s0:s1], in_=pairs[g, u][:].indirect(entries(s0, s1)))
 
-        def interleave(g, s0, s1, tag):
-            grouped[g, s0] = keep.tile([P, 2 * (s1 - s0)], U32, name=f"grouped{g}_{s0}", tag=tag, align_bytes=64)
+        def interleave(g, s0, s1, grouped):
             nc.scalar.copy(
-                out=grouped[g, s0][:].rearrange("p (s u) -> p s u", u=2),
+                out=grouped.rearrange("p (s u) -> p s u", u=2),
                 in_=picked[g][:, :, s0:s1].rearrange("p u s -> p s u"),
             )
 
-        def quantise(g, s0, s1):
-            nc.vector.quantize_mx(
-                out=x_codes[:, g, s0:s1].bitcast(FP8X4),
-                scales=x_planes[:, g, s0:s1],
-                in_=grouped[g, s0][:].bitcast(BF16),
-            )
+        def quantise(g, s0, s1, grouped, codes):
+            nc.vector.quantize_mx(out=codes.bitcast(FP8X4), scales=x_planes[:, g, s0:s1], in_=grouped.bitcast(BF16))
 
-        last = PASSES - 1
         cast(0, 0)
         for g in range(PASSES):
             gather(g, 0, 0, S)
             if g > 0:
-                quantise(g - 1, 0, S)
+                end = C if g == LAST else S
+                quantise(g - 1, 0, end, whole[:, 0 : 2 * end], x_codes[:, g - 1, 0:end])
             cast(g, 1)
-            if g < last:
+            if g < LAST:
                 gather(g, 1, 0, S)
                 cast(g + 1, 0)
-                interleave(g, 0, S, f"raw{g + 1}0")
-        cuts = [(0, FIRST), (FIRST, C), (C, S)]
-        for s0, s1 in cuts:
-            gather(last, 1, s0, s1)
-        for s0, s1 in cuts:
-            interleave(last, s0, s1, f"grouped{s0}")
-            quantise(last, s0, s1)
+                whole = keep.tile([P, 2 * S], U32, name=f"whole{g}", tag=f"raw{g + 1}0", align_bytes=64)
+                interleave(g, 0, S, whole[:])
 
-        units = [(b, s0, s1) for s0, s1 in cuts for b in range(BLOCKS)]
-        for b, s0, s1 in units:
-            rows = slice(b * P, (b + 1) * P)
-            acc = psum.tile([P, s1 - s0], F32, name=f"acc{b}_{s0}")
-            for e in range(E):
-                c0, c1 = max(s0, e * C), min(s1, (e + 1) * C)
-                if c0 >= c1:
-                    continue
+        for s0, s1 in CUTS:
+            gather(LAST, 1, s0, s1)
+        parts = []
+        for s0, s1 in CUTS:
+            part = keep.tile([P, 2 * (s1 - s0)], U32, name=f"part{s0}", tag=f"part{s0}", align_bytes=64)
+            interleave(LAST, s0, s1, part[:])
+            parts.append(part)
+        for (s0, s1), part in zip(CUTS[:2], parts):
+            quantise(LAST, s0, s1, part[:], x_codes[:, LAST, s0:s1])
+        late_codes = keep.tile([P, C], U32, name="late_codes", tag=f"part{CUTS[1][0]}", align_bytes=64)
+        quantise(LAST - 1, C, S, whole[:, 2 * C : 2 * S], late_codes[:])
+        quantise(LAST, C, S, parts[2][:], x_codes[:, LAST, C:S])
+
+        for s0, s1 in CUTS:
+            e = s0 // C
+            for b in range(BLOCKS):
+                features = slice(b * P, (b + 1) * P)
+                sums = psum.tile([P, s1 - s0], F32, name=f"sums{b}_{s0}")
                 for g in range(PASSES):
+                    codes = late_codes[:] if (e, g) == (1, LAST - 1) else x_codes[:, g, s0:s1]
                     nc.tensor.matmul_mx(
-                        out=acc[:, c0 - s0 : c1 - s0],
-                        lhsT=w_codes[:, e, g, rows].bitcast(FP8X4),
-                        lhsT_scale=w_planes[:, e * PASSES + g, rows],
-                        rhs=x_codes[:, g, c0:c1].bitcast(FP8X4),
-                        rhs_scale=x_planes[:, g, c0:c1],
+                        out=sums[:],
+                        lhsT=w_codes[:, e, g, features].bitcast(FP8X4),
+                        lhsT_scale=w_planes[:, e * PASSES + g, features],
+                        rhs=codes.bitcast(FP8X4),
+                        rhs_scale=x_planes[:, g, s0:s1],
                         start=(g == 0),
-                        stop=(g == PASSES - 1),
+                        stop=(g == LAST),
                     )
-            y = keep.tile([P, s1 - s0], F32, name=f"y{b}_{s0}")
-            nc.scalar.copy(out=y[:], in_=acc[:])
-            nc.vector.tensor_tensor(
-                out=windows[b][:].indirect(offsets[:, s0 // 16 : s1 // 16]),
-                in0=y[:],
-                in1=gates[:, s0:s1],
-                op=MULT,
-            )
-            if s1 == S:
-                nc.sync.dma_start(out[b * P : (b + 1) * P, :], windows[b][:])
+                y = keep.tile([P, s1 - s0], F32, name=f"y{b}_{s0}")
+                nc.scalar.copy(out=y[:], in_=sums[:])
+                nc.vector.tensor_tensor(
+                    out=windows[b][:].indirect(entries(s0, s1)), in0=y[:], in1=gates[:, s0:s1], op=MULT
+                )
+                if s1 == S:
+                    nc.sync.dma_start(out[features, :], windows[b][:])

@@ -22,7 +22,7 @@ FP8X4 = mybir.dt.float8_e4m3fn_x4
 MULT = mybir.AluOpType.mult
 
 CUTS = [(0, C // 2), (C // 2, C), (C, S)]
-ON_VECTOR = [672, 600, 600, 480, 520, 560]
+ON_VECTOR = [672, 600, 560, 464, 416, 384]
 RUN = 4
 
 
@@ -94,18 +94,19 @@ def tile_routed_moe_kernel(tc, xT, w_words, w_scales, gate, offs, out):
         def quantise(g, s0, s1, grouped, codes):
             nc.vector.quantize_mx(out=codes.bitcast(FP8X4), scales=x_planes[:, g, s0:s1], in_=grouped.bitcast(BF16))
 
-        cast(0, 0)
+        halves = {}
         for g in range(PASSES):
-            gather(g, 0, 0, S)
-            if g > 0:
-                end = C if g == LAST else S
-                quantise(g - 1, 0, end, whole[:, 0 : 2 * end], x_codes[:, g - 1, 0:end])
-            cast(g, 1)
-            if g < LAST:
-                gather(g, 1, 0, S)
-                cast(g + 1, 0)
-                whole = keep.tile([P, 2 * S], U32, name=f"whole{g}", tag=f"raw{g + 1}0", align_bytes=64)
-                interleave(g, 0, S, whole[:])
+            for u in range(2):
+                cast(g, u)
+                before = (g - 1, 0) if u == 1 else (g - 2, 1)
+                if before in halves:
+                    bg, be = before
+                    quantise(bg, be * C, (be + 1) * C, halves[before][:], x_codes[:, bg, be * C : (be + 1) * C])
+                if g > 0:
+                    halves[g - 1, u] = keep.tile([P, 2 * C], U32, name=f"half{g}{u}", tag=f"raw{g}{u}", align_bytes=64)
+                    interleave(g - 1, u * C, (u + 1) * C, halves[g - 1, u][:])
+                if (g, u) != (LAST, 1):
+                    gather(g, u, 0, S)
 
         for s0, s1 in CUTS:
             gather(LAST, 1, s0, s1)
@@ -117,7 +118,7 @@ def tile_routed_moe_kernel(tc, xT, w_words, w_scales, gate, offs, out):
         for (s0, s1), part in zip(CUTS[:2], parts):
             quantise(LAST, s0, s1, part[:], x_codes[:, LAST, s0:s1])
         late_codes = keep.tile([P, C], U32, name="late_codes", tag=f"part{CUTS[1][0]}", align_bytes=64)
-        quantise(LAST - 1, C, S, whole[:, 2 * C : 2 * S], late_codes[:])
+        quantise(LAST - 1, C, S, halves[LAST - 1, 1][:], late_codes[:])
         quantise(LAST, C, S, parts[2][:], x_codes[:, LAST, C:S])
 
         for s0, s1 in CUTS:

@@ -23,7 +23,6 @@ MULT = mybir.AluOpType.mult
 
 CUTS = [(0, C // 2), (C // 2, C), (C, S)]
 ON_VECTOR = [672, 600, 560, 464, 416, 384]
-RUN = 4
 
 
 def tile_routed_moe_kernel(tc, xT, w_words, w_scales, gate, offs, out):
@@ -76,9 +75,9 @@ def tile_routed_moe_kernel(tc, xT, w_words, w_scales, gate, offs, out):
 
         def cast(g, u):
             pairs[g, u] = keep.tile([P, T], U32, name=f"pairs{g}{u}", align_bytes=64)
-            dst = pairs[g, u][:].bitcast(BF16).rearrange("p (c i r) -> p c r i", i=RUN, r=2)
-            src = raws[g, u][:].rearrange("p r (c i) -> p c r i", i=RUN)
-            runs = ON_VECTOR[2 * g + u] // RUN
+            dst = pairs[g, u][:].bitcast(BF16).rearrange("p (t r) -> p t r", r=2)
+            src = raws[g, u][:].rearrange("p r t -> p t r")
+            runs = ON_VECTOR[2 * g + u]
             nc.vector.tensor_copy(out=dst[:, :runs], in_=src[:, :runs])
             nc.scalar.copy(out=dst[:, runs:], in_=src[:, runs:])
 

@@ -22,7 +22,10 @@ FP8X4 = mybir.dt.float8_e4m3fn_x4
 MULT = mybir.AluOpType.mult
 
 CUTS = [(0, C // 2), (C // 2, C), (C, S)]
-ON_VECTOR = [672, 600, 560, 464, 416, 384]
+ON_VECTOR = [672, 600, 544, 560, 520, 416]
+LOADS = 2 * PASSES
+LATE = 16
+MIDDLE = 160
 
 
 def tile_routed_moe_kernel(tc, xT, w_words, w_scales, gate, offs, out):
@@ -40,15 +43,12 @@ def tile_routed_moe_kernel(tc, xT, w_words, w_scales, gate, offs, out):
             windows.append(window)
 
         x_rows = xT.rearrange("(g p u r) t -> g u p r t", p=P, u=2, r=2)
-        raws = {}
+        raw = keep.tile([P, LOADS, 2, T], F32, name="raw", align_bytes=64)
         offsets = keep.tile([P, S // 16], U16, name="offsets")
-        for g in range(PASSES):
-            for u in range(2):
-                raw = keep.tile([P, 2, T], F32, name=f"raw{g}{u}", tag=f"raw{g}{u}", align_bytes=64)
-                nc.sync.dma_start(raw[:], x_rows[g, u])
-                raws[g, u] = raw
-                if (g, u) == (0, 0):
-                    nc.sync.dma_start(offsets[:], offs)
+        for i in range(LOADS):
+            nc.sync.dma_start(raw[:, i], x_rows[i // 2, i % 2])
+            if i == 0:
+                nc.sync.dma_start(offsets[:], offs)
 
         w_codes = keep.tile([P, E, PASSES, N], U32, name="w_codes", align_bytes=64)
         for q in range(4):
@@ -65,24 +65,22 @@ def tile_routed_moe_kernel(tc, xT, w_words, w_scales, gate, offs, out):
             if e == 0:
                 nc.sync.dma_start(gates[:], gate[0:P, :])
 
-        x_codes = keep.tile([P, PASSES, S], U32, name="x_codes", align_bytes=64)
         x_planes = keep.tile([P, PASSES, S], U8, name="x_planes", align_bytes=64)
         picked = [keep.tile([P, 2, S], U32, name=f"picked{g}", align_bytes=64) for g in range(PASSES)]
-        pairs = {}
+        pairs = [keep.tile([P, T], U32, name=f"pairs{i}", align_bytes=64) for i in range(LOADS)]
+        x_codes = keep.tile([P, PASSES, S], U32, name="x_codes", align_bytes=64)
+        raw_words = raw[:].rearrange("p i r t -> p (i r t)").bitcast(U32)
 
         def entries(s0, s1):
             return offsets[:, s0 // 16 : s1 // 16]
 
-        def cast(g, u):
-            pairs[g, u] = keep.tile([P, T], U32, name=f"pairs{g}{u}", align_bytes=64)
-            dst = pairs[g, u][:].bitcast(BF16).rearrange("p (t r) -> p t r", r=2)
-            src = raws[g, u][:].rearrange("p r t -> p t r")
-            runs = ON_VECTOR[2 * g + u]
-            nc.vector.tensor_copy(out=dst[:, :runs], in_=src[:, :runs])
-            nc.scalar.copy(out=dst[:, runs:], in_=src[:, runs:])
+        def cast(copy, i, t0, t1):
+            dst = pairs[i][:].bitcast(BF16).rearrange("p (t r) -> p t r", r=2)
+            src = raw[:, i].rearrange("p r t -> p t r")
+            copy(out=dst[:, t0:t1], in_=src[:, t0:t1])
 
-        def gather(g, u, s0, s1):
-            nc.vector.tensor_copy(out=picked[g][:, u, s0:s1], in_=pairs[g, u][:].indirect(entries(s0, s1)))
+        def gather(i, s0, s1):
+            nc.vector.tensor_copy(out=picked[i // 2][:, i % 2, s0:s1], in_=pairs[i][:].indirect(entries(s0, s1)))
 
         def interleave(g, s0, s1, grouped):
             nc.scalar.copy(
@@ -90,35 +88,42 @@ def tile_routed_moe_kernel(tc, xT, w_words, w_scales, gate, offs, out):
                 in_=picked[g][:, :, s0:s1].rearrange("p u s -> p s u"),
             )
 
-        def quantise(g, s0, s1, grouped, codes):
-            nc.vector.quantize_mx(out=codes.bitcast(FP8X4), scales=x_planes[:, g, s0:s1], in_=grouped.bitcast(BF16))
+        def quantise(g, s0, s1, grouped):
+            nc.vector.quantize_mx(
+                out=x_codes[:, g, s0:s1].bitcast(FP8X4), scales=x_planes[:, g, s0:s1], in_=grouped.bitcast(BF16)
+            )
 
-        halves = {}
-        for g in range(PASSES):
-            for u in range(2):
-                cast(g, u)
-                before = (g - 1, 0) if u == 1 else (g - 2, 1)
-                if before in halves:
-                    bg, be = before
-                    quantise(bg, be * C, (be + 1) * C, halves[before][:], x_codes[:, bg, be * C : (be + 1) * C])
-                if g > 0:
-                    halves[g - 1, u] = keep.tile([P, 2 * C], U32, name=f"half{g}{u}", tag=f"raw{g}{u}", align_bytes=64)
-                    interleave(g - 1, u * C, (u + 1) * C, halves[g - 1, u][:])
-                if (g, u) != (LAST, 1):
-                    gather(g, u, 0, S)
+        stretches = {2: (0, 0, C), 3: (0, C, S), 4: (1, 0, S)}
+
+        def words_behind(i):
+            g, s0, s1 = stretches[i]
+            end = (i + 1) * 2 * T + 2 * LATE
+            return raw_words[:, end - 2 * (s1 - s0) : end]
+
+        for i in range(LOADS):
+            split = T - ON_VECTOR[i]
+            cast(nc.vector.tensor_copy, i, split, T)
+            if i - 1 in stretches:
+                g, s0, s1 = stretches[i - 1]
+                cast(nc.scalar.copy, i, 0, 2 * LATE)
+                cast(nc.scalar.copy, i, 2 * LATE, MIDDLE)
+                interleave(g, s1 - LATE, s1, words_behind(i - 1)[:, 2 * (s1 - s0 - LATE) :])
+                cast(nc.scalar.copy, i, MIDDLE, split)
+                quantise(g, s0, s1, words_behind(i - 1))
+            else:
+                cast(nc.scalar.copy, i, 0, split)
+            if i < LOADS - 1:
+                gather(i, 0, S)
+            if i in stretches:
+                g, s0, s1 = stretches[i]
+                interleave(g, s0, s1 - LATE, words_behind(i)[:, : 2 * (s1 - s0 - LATE)])
 
         for s0, s1 in CUTS:
-            gather(LAST, 1, s0, s1)
-        parts = []
+            gather(LOADS - 1, s0, s1)
         for s0, s1 in CUTS:
-            part = keep.tile([P, 2 * (s1 - s0)], U32, name=f"part{s0}", tag=f"part{s0}", align_bytes=64)
+            part = keep.tile([P, 2 * (s1 - s0)], U32, name=f"part{s0}", align_bytes=64)
             interleave(LAST, s0, s1, part[:])
-            parts.append(part)
-        for (s0, s1), part in zip(CUTS[:2], parts):
-            quantise(LAST, s0, s1, part[:], x_codes[:, LAST, s0:s1])
-        late_codes = keep.tile([P, C], U32, name="late_codes", tag=f"part{CUTS[1][0]}", align_bytes=64)
-        quantise(LAST - 1, C, S, halves[LAST - 1, 1][:], late_codes[:])
-        quantise(LAST, C, S, parts[2][:], x_codes[:, LAST, C:S])
+            quantise(LAST, s0, s1, part[:])
 
         for s0, s1 in CUTS:
             e = s0 // C
@@ -126,12 +131,11 @@ def tile_routed_moe_kernel(tc, xT, w_words, w_scales, gate, offs, out):
                 features = slice(b * P, (b + 1) * P)
                 sums = psum.tile([P, s1 - s0], F32, name=f"sums{b}_{s0}")
                 for g in range(PASSES):
-                    codes = late_codes[:] if (e, g) == (1, LAST - 1) else x_codes[:, g, s0:s1]
                     nc.tensor.matmul_mx(
                         out=sums[:],
                         lhsT=w_codes[:, e, g, features].bitcast(FP8X4),
                         lhsT_scale=w_planes[:, e * PASSES + g, features],
-                        rhs=codes.bitcast(FP8X4),
+                        rhs=x_codes[:, g, s0:s1].bitcast(FP8X4),
                         rhs_scale=x_planes[:, g, s0:s1],
                         start=(g == 0),
                         stop=(g == LAST),

@@ -22,7 +22,8 @@ FP8X4 = mybir.dt.float8_e4m3fn_x4
 MULT = mybir.AluOpType.mult
 
 CUTS = [(0, C // 2), (C // 2, C), (C, S)]
-ON_VECTOR = [672, 600, 544, 560, 520, 416]
+ON_VECTOR = [672, 640, 608, 616, 576, 592]
+LAST_AT = {0: S, C // 2: S + C, C: S}
 LOADS = 2 * PASSES
 LATE = 16
 MIDDLE = 160
@@ -66,9 +67,14 @@ def tile_routed_moe_kernel(tc, xT, w_words, w_scales, gate, offs, out):
                 nc.sync.dma_start(gates[:], gate[0:P, :])
 
         x_planes = keep.tile([P, PASSES, S], U8, name="x_planes", align_bytes=64)
-        picked = [keep.tile([P, 2, S], U32, name=f"picked{g}", align_bytes=64) for g in range(PASSES)]
+        picked = [keep.tile([P, 2, S], U32, name=f"picked{g}", align_bytes=64) for g in range(LAST)]
+        last_picked = keep.tile([P, 3 * S], U32, name="last_picked", align_bytes=64)
         pairs = [keep.tile([P, T], U32, name=f"pairs{i}", align_bytes=64) for i in range(LOADS)]
-        x_codes = keep.tile([P, PASSES, S], U32, name="x_codes", align_bytes=64)
+        x_codes = keep.tile([P, LAST, S], U32, name="x_codes", align_bytes=64)
+        last_codes = {
+            s0: keep.tile([P, s1 - s0], U32, name=f"last_codes{s0}", tag=f"last_codes{s0}", align_bytes=64)
+            for s0, s1 in CUTS
+        }
         raw_words = raw[:].rearrange("p i r t -> p (i r t)").bitcast(U32)
 
         def entries(s0, s1):
@@ -79,21 +85,30 @@ def tile_routed_moe_kernel(tc, xT, w_words, w_scales, gate, offs, out):
             src = raw[:, i].rearrange("p r t -> p t r")
             copy(out=dst[:, t0:t1], in_=src[:, t0:t1])
 
+        def rows_of(g, s0, s1):
+            if g < LAST:
+                return picked[g][:, :, s0:s1]
+            step = LAST_AT[s0] - s0
+            return last_picked[:, s0 : s0 + 2 * step].rearrange("p (u s) -> p u s", u=2)[:, :, : s1 - s0]
+
         def gather(i, s0, s1):
-            nc.vector.tensor_copy(out=picked[i // 2][:, i % 2, s0:s1], in_=pairs[i][:].indirect(entries(s0, s1)))
+            nc.vector.tensor_copy(out=rows_of(i // 2, s0, s1)[:, i % 2], in_=pairs[i][:].indirect(entries(s0, s1)))
 
         def interleave(g, s0, s1, grouped):
             nc.scalar.copy(
                 out=grouped.rearrange("p (s u) -> p s u", u=2),
-                in_=picked[g][:, :, s0:s1].rearrange("p u s -> p s u"),
+                in_=rows_of(g, s0, s1).rearrange("p u s -> p s u"),
             )
+
+        def codes_of(g, s0, s1):
+            return x_codes[:, g, s0:s1] if g < LAST else last_codes[s0][:]
 
         def quantise(g, s0, s1, grouped):
             nc.vector.quantize_mx(
-                out=x_codes[:, g, s0:s1].bitcast(FP8X4), scales=x_planes[:, g, s0:s1], in_=grouped.bitcast(BF16)
+                out=codes_of(g, s0, s1).bitcast(FP8X4), scales=x_planes[:, g, s0:s1], in_=grouped.bitcast(BF16)
             )
 
-        stretches = {2: (0, 0, C), 3: (0, C, S), 4: (1, 0, S)}
+        stretches = {2: (0, 0, C), 3: (0, C, S), 4: (1, 0, C)}
 
         def words_behind(i):
             g, s0, s1 = stretches[i]
@@ -118,15 +133,23 @@ def tile_routed_moe_kernel(tc, xT, w_words, w_scales, gate, offs, out):
                 g, s0, s1 = stretches[i]
                 interleave(g, s0, s1 - LATE, words_behind(i)[:, : 2 * (s1 - s0 - LATE)])
 
-        for s0, s1 in CUTS:
+        late = raw_words[:, LOADS * 2 * T - 2 * C :]
+        interleave(LAST - 1, C, S, late)
+        parts = [keep.tile([P, 2 * (s1 - s0)], U32, name=f"part{s0}", align_bytes=64) for s0, s1 in CUTS[:2]]
+        for (s0, s1), part in zip(CUTS[:2], parts):
             gather(LOADS - 1, s0, s1)
-        for s0, s1 in CUTS:
-            part = keep.tile([P, 2 * (s1 - s0)], U32, name=f"part{s0}", align_bytes=64)
             interleave(LAST, s0, s1, part[:])
-            quantise(LAST, s0, s1, part[:])
+        quantise(LAST - 1, C, S, late)
+        quantise(LAST, *CUTS[0], parts[0][:])
+        gather(LOADS - 1, *CUTS[2])
+        quantise(LAST, *CUTS[1], parts[1][:])
 
         for s0, s1 in CUTS:
             e = s0 // C
+            if s0 == CUTS[1][0]:
+                part = keep.tile([P, 2 * C], U32, name="long_part", tag="last_codes0", align_bytes=64)
+                interleave(LAST, C, S, part[:])
+                quantise(LAST, C, S, part[:])
             for b in range(BLOCKS):
                 features = slice(b * P, (b + 1) * P)
                 sums = psum.tile([P, s1 - s0], F32, name=f"sums{b}_{s0}")
@@ -135,7 +158,7 @@ def tile_routed_moe_kernel(tc, xT, w_words, w_scales, gate, offs, out):
                         out=sums[:],
                         lhsT=w_codes[:, e, g, features].bitcast(FP8X4),
                         lhsT_scale=w_planes[:, e * PASSES + g, features],
-                        rhs=x_codes[:, g, s0:s1].bitcast(FP8X4),
+                        rhs=codes_of(g, s0, s1).bitcast(FP8X4),
                         rhs_scale=x_planes[:, g, s0:s1],
                         start=(g == 0),
                         stop=(g == LAST),

@@ -5,7 +5,8 @@ import concourse.mybir as mybir
 K, T, E, C, N = 1536, 1024, 2, 256, 256
 S = E * C
 P = 128
-PASSES = K // 512
+PACK = 4
+PASSES = K // (P * PACK)
 LAST = PASSES - 1
 BLOCKS = N // P
 
@@ -20,13 +21,13 @@ U16 = mybir.dt.uint16
 U8 = mybir.dt.uint8
 FP8X4 = mybir.dt.float8_e4m3fn_x4
 MULT = mybir.AluOpType.mult
+COPY = mybir.ActivationFunctionType.Copy
 
+LOADS = [(0, 0, 2), (0, 2, 2), (1, 2, 2), (1, 0, 2), (2, 0, 2), (2, 3, 1), (2, 2, 1)]
+FIRST_PLACE = [0, 3, 0]
+SHARED_PLACE = 3
 CUTS = [(0, C // 2), (C // 2, C), (C, S)]
-ON_VECTOR = [672, 640, 608, 616, 576, 592]
-LAST_AT = {0: S, C // 2: S + C, C: S}
-LOADS = 2 * PASSES
-LATE = 16
-MIDDLE = 160
+SCALAR_END = C + C // 2
 
 
 def tile_routed_moe_kernel(tc, xT, w_words, w_scales, gate, offs, out):
@@ -37,17 +38,15 @@ def tile_routed_moe_kernel(tc, xT, w_words, w_scales, gate, offs, out):
 
         w_planes = keep.tile([P, E * PASSES, N], U8, name="w_planes", align_bytes=64)
         nc.vector.memset(w_planes[:].rearrange("p a n -> p (a n)").bitcast(I32), 0)
-        windows = []
-        for b in range(BLOCKS):
-            window = keep.tile([P, T], F32, name=f"window{b}")
-            nc.vector.memset(window[:], 0.0)
-            windows.append(window)
+        windows = [keep.tile([P, T], F32, name=f"window{b}") for b in range(BLOCKS)]
+        nc.vector.memset(windows[1][:], 0.0)
+        nc.scalar.activation(windows[0][:], windows[1][:], COPY)
 
-        x_rows = xT.rearrange("(g p u r) t -> g u p r t", p=P, u=2, r=2)
-        raw = keep.tile([P, LOADS, 2, T], F32, name="raw", align_bytes=64)
+        x_rows = xT.rearrange("(g p t) n -> g p t n", p=P, t=PACK)
+        raw = keep.tile([P, PASSES, PACK, T], F32, name="raw", align_bytes=64)
         offsets = keep.tile([P, S // 16], U16, name="offsets")
-        for i in range(LOADS):
-            nc.sync.dma_start(raw[:, i], x_rows[i // 2, i % 2])
+        for i, (g, t0, count) in enumerate(LOADS):
+            nc.sync.dma_start(raw[:, g, t0 : t0 + count], x_rows[g, :, t0 : t0 + count])
             if i == 0:
                 nc.sync.dma_start(offsets[:], offs)
 
@@ -66,107 +65,105 @@ def tile_routed_moe_kernel(tc, xT, w_words, w_scales, gate, offs, out):
             if e == 0:
                 nc.sync.dma_start(gates[:], gate[0:P, :])
 
+        picked = keep.tile([P, 2 * PACK - 1, S], F32, name="picked", align_bytes=64)
+        grouped = keep.tile([P, PASSES, S * PACK], BF16, name="grouped", align_bytes=64)
+        x_codes = keep.tile([P, PASSES, S], U32, name="x_codes", align_bytes=64)
         x_planes = keep.tile([P, PASSES, S], U8, name="x_planes", align_bytes=64)
-        picked = [keep.tile([P, 2, S], U32, name=f"picked{g}", align_bytes=64) for g in range(LAST)]
-        last_picked = keep.tile([P, 3 * S], U32, name="last_picked", align_bytes=64)
-        pairs = [keep.tile([P, T], U32, name=f"pairs{i}", align_bytes=64) for i in range(LOADS)]
-        x_codes = keep.tile([P, LAST, S], U32, name="x_codes", align_bytes=64)
-        last_codes = {
-            s0: keep.tile([P, s1 - s0], U32, name=f"last_codes{s0}", tag=f"last_codes{s0}", align_bytes=64)
-            for s0, s1 in CUTS
-        }
-        raw_words = raw[:].rearrange("p i r t -> p (i r t)").bitcast(U32)
 
         def entries(s0, s1):
             return offsets[:, s0 // 16 : s1 // 16]
 
-        def cast(copy, i, t0, t1):
-            dst = pairs[i][:].bitcast(BF16).rearrange("p (t r) -> p t r", r=2)
-            src = raw[:, i].rearrange("p r t -> p t r")
-            copy(out=dst[:, t0:t1], in_=src[:, t0:t1])
+        def gather_on_vector(g, t, s0, s1):
+            nc.vector.tensor_copy(out=picked[:, FIRST_PLACE[g] + t, s0:s1], in_=raw[:, g, t].indirect(entries(s0, s1)))
 
-        def rows_of(g, s0, s1):
-            if g < LAST:
-                return picked[g][:, :, s0:s1]
-            step = LAST_AT[s0] - s0
-            return last_picked[:, s0 : s0 + 2 * step].rearrange("p (u s) -> p u s", u=2)[:, :, : s1 - s0]
+        def gather_on_scalar(g, t, s0, s1):
+            nc.scalar.activation(picked[:, FIRST_PLACE[g] + t, s0:s1], raw[:, g, t].indirect(entries(s0, s1)), COPY)
 
-        def gather(i, s0, s1):
-            nc.vector.tensor_copy(out=rows_of(i // 2, s0, s1)[:, i % 2], in_=pairs[i][:].indirect(entries(s0, s1)))
-
-        def interleave(g, s0, s1, grouped):
-            nc.scalar.copy(
-                out=grouped.rearrange("p (s u) -> p s u", u=2),
-                in_=rows_of(g, s0, s1).rearrange("p u s -> p s u"),
+        def interleave(copy, g, s0, s1):
+            rows = picked[:, FIRST_PLACE[g] : FIRST_PLACE[g] + PACK, s0:s1]
+            copy(
+                out=grouped[:, g, PACK * s0 : PACK * s1].rearrange("p (c i t) -> p c t i", i=4, t=PACK),
+                in_=rows.rearrange("p t (c i) -> p c t i", i=4),
             )
 
-        def codes_of(g, s0, s1):
-            return x_codes[:, g, s0:s1] if g < LAST else last_codes[s0][:]
-
-        def quantise(g, s0, s1, grouped):
+        def quantise(g, s0, s1):
             nc.vector.quantize_mx(
-                out=codes_of(g, s0, s1).bitcast(FP8X4), scales=x_planes[:, g, s0:s1], in_=grouped.bitcast(BF16)
+                out=x_codes[:, g, s0:s1].bitcast(FP8X4),
+                scales=x_planes[:, g, s0:s1],
+                in_=grouped[:, g, PACK * s0 : PACK * s1],
             )
 
-        stretches = {2: (0, 0, C), 3: (0, C, S), 4: (1, 0, C)}
+        for g, t0, count in LOADS[:-1]:
+            closing = g < LAST and t0 <= SHARED_PLACE - FIRST_PLACE[g] < t0 + count
+            for t in range(t0, t0 + count):
+                if FIRST_PLACE[g] + t == SHARED_PLACE:
+                    gather_on_vector(g, t, 0, S)
+                elif closing:
+                    for e in range(E):
+                        gather_on_scalar(g, t, e * C, (e + 1) * C)
+                else:
+                    gather_on_scalar(g, t, 0, S)
+            if closing:
+                for e in range(E):
+                    interleave(nc.vector.tensor_copy, g, e * C, (e + 1) * C)
+                for e in range(E):
+                    quantise(g, e * C, (e + 1) * C)
 
-        def words_behind(i):
-            g, s0, s1 = stretches[i]
-            end = (i + 1) * 2 * T + 2 * LATE
-            return raw_words[:, end - 2 * (s1 - s0) : end]
+        groups = [(c, b) for c in range(len(CUTS)) for b in range(BLOCKS)]
+        sums = {(c, b): psum.tile([P, CUTS[c][1] - CUTS[c][0]], F32, name=f"sums{c}_{b}") for c, b in groups}
+        y = {(c, b): keep.tile([P, CUTS[c][1] - CUTS[c][0]], F32, name=f"y{c}_{b}") for c, b in groups}
 
-        for i in range(LOADS):
-            split = T - ON_VECTOR[i]
-            cast(nc.vector.tensor_copy, i, split, T)
-            if i - 1 in stretches:
-                g, s0, s1 = stretches[i - 1]
-                cast(nc.scalar.copy, i, 0, 2 * LATE)
-                cast(nc.scalar.copy, i, 2 * LATE, MIDDLE)
-                interleave(g, s1 - LATE, s1, words_behind(i - 1)[:, 2 * (s1 - s0 - LATE) :])
-                cast(nc.scalar.copy, i, MIDDLE, split)
-                quantise(g, s0, s1, words_behind(i - 1))
-            else:
-                cast(nc.scalar.copy, i, 0, split)
-            if i < LOADS - 1:
-                gather(i, 0, S)
-            if i in stretches:
-                g, s0, s1 = stretches[i]
-                interleave(g, s0, s1 - LATE, words_behind(i)[:, : 2 * (s1 - s0 - LATE)])
-
-        late = raw_words[:, LOADS * 2 * T - 2 * C :]
-        interleave(LAST - 1, C, S, late)
-        parts = [keep.tile([P, 2 * (s1 - s0)], U32, name=f"part{s0}", align_bytes=64) for s0, s1 in CUTS[:2]]
-        for (s0, s1), part in zip(CUTS[:2], parts):
-            gather(LOADS - 1, s0, s1)
-            interleave(LAST, s0, s1, part[:])
-        quantise(LAST - 1, C, S, late)
-        quantise(LAST, *CUTS[0], parts[0][:])
-        gather(LOADS - 1, *CUTS[2])
-        quantise(LAST, *CUTS[1], parts[1][:])
-
-        for s0, s1 in CUTS:
+        def multiply(c, b, passes):
+            s0, s1 = CUTS[c]
             e = s0 // C
-            if s0 == CUTS[1][0]:
-                part = keep.tile([P, 2 * C], U32, name="long_part", tag="last_codes0", align_bytes=64)
-                interleave(LAST, C, S, part[:])
-                quantise(LAST, C, S, part[:])
-            for b in range(BLOCKS):
-                features = slice(b * P, (b + 1) * P)
-                sums = psum.tile([P, s1 - s0], F32, name=f"sums{b}_{s0}")
-                for g in range(PASSES):
-                    nc.tensor.matmul_mx(
-                        out=sums[:],
-                        lhsT=w_codes[:, e, g, features].bitcast(FP8X4),
-                        lhsT_scale=w_planes[:, e * PASSES + g, features],
-                        rhs=codes_of(g, s0, s1).bitcast(FP8X4),
-                        rhs_scale=x_planes[:, g, s0:s1],
-                        start=(g == 0),
-                        stop=(g == LAST),
-                    )
-                y = keep.tile([P, s1 - s0], F32, name=f"y{b}_{s0}")
-                nc.scalar.copy(out=y[:], in_=sums[:])
-                nc.vector.tensor_tensor(
-                    out=windows[b][:].indirect(entries(s0, s1)), in0=y[:], in1=gates[:, s0:s1], op=MULT
+            features = slice(b * P, (b + 1) * P)
+            for g in passes:
+                nc.tensor.matmul_mx(
+                    out=sums[c, b][:],
+                    lhsT=w_codes[:, e, g, features].bitcast(FP8X4),
+                    lhsT_scale=w_planes[:, e * PASSES + g, features],
+                    rhs=x_codes[:, g, s0:s1].bitcast(FP8X4),
+                    rhs_scale=x_planes[:, g, s0:s1],
+                    start=(g == 0),
+                    stop=(g == LAST),
                 )
-                if s1 == S:
-                    nc.sync.dma_start(out[features, :], windows[b][:])
+
+        def times_gate(c):
+            s0, s1 = CUTS[c]
+            nc.vector.tensor_tensor(out=y[c, 0][:], in0=sums[c, 0][:], in1=gates[:, s0:s1], op=MULT)
+
+        def scatter_on_scalar(c):
+            nc.scalar.activation(windows[0][:].indirect(entries(*CUTS[c])), y[c, 0][:], COPY)
+
+        def scatter_on_vector(c):
+            s0, s1 = CUTS[c]
+            nc.vector.tensor_tensor(out=windows[1][:].indirect(entries(s0, s1)), in0=y[c, 1][:], in1=gates[:, s0:s1], op=MULT)
+
+        last_row = LOADS[-1][1]
+        gather_on_scalar(LAST, last_row, *CUTS[0])
+        gather_on_vector(LAST, last_row, *CUTS[1])
+        gather_on_scalar(LAST, last_row, *CUTS[2])
+        interleave(nc.vector.tensor_copy, LAST, *CUTS[0])
+        interleave(nc.vector.tensor_copy, LAST, *CUTS[1])
+        interleave(nc.scalar.copy, LAST, C, SCALAR_END)
+        quantise(LAST, *CUTS[0])
+        quantise(LAST, *CUTS[1])
+        interleave(nc.vector.tensor_copy, LAST, SCALAR_END, S)
+
+        for c, b in groups[:3]:
+            multiply(c, b, range(LAST))
+        for c, b in groups[:3]:
+            multiply(c, b, [LAST])
+        multiply(*groups[3], range(PASSES))
+        times_gate(0)
+        quantise(LAST, *CUTS[2])
+        for c, b in groups[4:]:
+            multiply(c, b, range(PASSES))
+        for c in range(len(CUTS)):
+            nc.scalar.copy(out=y[c, 1][:], in_=sums[c, 1][:])
+            scatter_on_scalar(c)
+            if c + 1 < len(CUTS):
+                times_gate(c + 1)
+            scatter_on_vector(c)
+        for b in range(BLOCKS):
+            nc.sync.dma_start(out[b * P : (b + 1) * P, :], windows[b][:])

@@ -23,11 +23,10 @@ FP8X4 = mybir.dt.float8_e4m3fn_x4
 MULT = mybir.AluOpType.mult
 COPY = mybir.ActivationFunctionType.Copy
 
-LOADS = [(0, 0, 2), (0, 2, 2), (1, 2, 2), (1, 0, 2), (2, 0, 2), (2, 3, 1), (2, 2, 1)]
+LOADS = [(0, 0, 2), (0, 2, 2), (1, 2, 2), (1, 0, 2), (2, 1, 2), (2, 3, 1), (2, 0, 1)]
 FIRST_PLACE = [0, 3, 0]
 SHARED_PLACE = 3
 CUTS = [(0, C // 2), (C // 2, C), (C, S)]
-SCALAR_END = C + C // 2
 
 
 def tile_routed_moe_kernel(tc, xT, w_words, w_scales, gate, offs, out):
@@ -67,7 +66,11 @@ def tile_routed_moe_kernel(tc, xT, w_words, w_scales, gate, offs, out):
 
         picked = keep.tile([P, 2 * PACK - 1, S], F32, name="picked", align_bytes=64)
         grouped = keep.tile([P, PASSES, S * PACK], BF16, name="grouped", align_bytes=64)
-        x_codes = keep.tile([P, PASSES, S], U32, name="x_codes", align_bytes=64)
+        x_codes = keep.tile([P, LAST, S], U32, name="x_codes", align_bytes=64)
+        last_codes = {
+            s0: keep.tile([P, s1 - s0], U32, name=f"last_codes{s0}", tag=f"last_codes{s0}", align_bytes=64)
+            for s0, s1 in CUTS[:2]
+        }
         x_planes = keep.tile([P, PASSES, S], U8, name="x_planes", align_bytes=64)
 
         def entries(s0, s1):
@@ -86,84 +89,104 @@ def tile_routed_moe_kernel(tc, xT, w_words, w_scales, gate, offs, out):
                 in_=rows.rearrange("p t (c i) -> p c t i", i=4),
             )
 
+        def codes_of(g, s0, s1):
+            return x_codes[:, g, s0:s1] if g < LAST else last_codes[s0][:]
+
         def quantise(g, s0, s1):
             nc.vector.quantize_mx(
-                out=x_codes[:, g, s0:s1].bitcast(FP8X4),
+                out=codes_of(g, s0, s1).bitcast(FP8X4),
                 scales=x_planes[:, g, s0:s1],
                 in_=grouped[:, g, PACK * s0 : PACK * s1],
             )
 
-        for g, t0, count in LOADS[:-1]:
-            closing = g < LAST and t0 <= SHARED_PLACE - FIRST_PLACE[g] < t0 + count
+        halves = [(e * C, (e + 1) * C) for e in range(E)]
+        for g, t0, count in LOADS[: 2 * LAST]:
+            closing = t0 <= SHARED_PLACE - FIRST_PLACE[g] < t0 + count
             for t in range(t0, t0 + count):
                 if FIRST_PLACE[g] + t == SHARED_PLACE:
                     gather_on_vector(g, t, 0, S)
                 elif closing:
-                    for e in range(E):
-                        gather_on_scalar(g, t, e * C, (e + 1) * C)
+                    for half in halves:
+                        gather_on_scalar(g, t, *half)
                 else:
                     gather_on_scalar(g, t, 0, S)
             if closing:
-                for e in range(E):
-                    interleave(nc.vector.tensor_copy, g, e * C, (e + 1) * C)
-                for e in range(E):
-                    quantise(g, e * C, (e + 1) * C)
+                for half in halves:
+                    interleave(nc.vector.tensor_copy, g, *half)
+                for half in halves:
+                    quantise(g, *half)
+
+        for half in halves:
+            for t in (1, 2):
+                gather_on_scalar(LAST, t, *half)
+        for half in halves:
+            gather_on_vector(LAST, 3, *half)
+        for s0, s1 in CUTS[:2]:
+            nc.vector.tensor_copy(
+                out=grouped[:, LAST, PACK * s0 : PACK * s1].rearrange("p (c i t) -> p c t i", i=4, t=PACK)[:, :, 1:],
+                in_=picked[:, 1:PACK, s0:s1].rearrange("p t (c i) -> p c t i", i=4),
+            )
+        for s0, s1 in CUTS[:2]:
+            nc.vector.tensor_copy(
+                out=grouped[:, LAST, PACK * s0 : PACK * s1 : PACK], in_=raw[:, LAST, 0].indirect(entries(s0, s1))
+            )
+        quantise(LAST, *CUTS[0])
+        quantise(LAST, *CUTS[1])
+        pieces = [(C, C + C // 2), (C + C // 2, S)]
+        for piece in pieces:
+            gather_on_scalar(LAST, 0, *piece)
+        for piece in pieces:
+            interleave(nc.scalar.copy, LAST, *piece)
 
         groups = [(c, b) for c in range(len(CUTS)) for b in range(BLOCKS)]
         sums = {(c, b): psum.tile([P, CUTS[c][1] - CUTS[c][0]], F32, name=f"sums{c}_{b}") for c, b in groups}
-        y = {(c, b): keep.tile([P, CUTS[c][1] - CUTS[c][0]], F32, name=f"y{c}_{b}") for c, b in groups}
+        y = [keep.tile([P, S], F32, name=f"y{b}") for b in range(BLOCKS)]
 
-        def multiply(c, b, passes):
+        def multiply(c, b):
             s0, s1 = CUTS[c]
             e = s0 // C
             features = slice(b * P, (b + 1) * P)
+            passes = list(range(PASSES)) if c == 0 else list(reversed(range(PASSES)))
             for g in passes:
                 nc.tensor.matmul_mx(
                     out=sums[c, b][:],
                     lhsT=w_codes[:, e, g, features].bitcast(FP8X4),
                     lhsT_scale=w_planes[:, e * PASSES + g, features],
-                    rhs=x_codes[:, g, s0:s1].bitcast(FP8X4),
+                    rhs=codes_of(g, s0, s1).bitcast(FP8X4),
                     rhs_scale=x_planes[:, g, s0:s1],
-                    start=(g == 0),
-                    stop=(g == LAST),
+                    start=(g == passes[0]),
+                    stop=(g == passes[-1]),
                 )
 
         def times_gate(c):
             s0, s1 = CUTS[c]
-            nc.vector.tensor_tensor(out=y[c, 0][:], in0=sums[c, 0][:], in1=gates[:, s0:s1], op=MULT)
+            nc.vector.tensor_tensor(out=y[0][:, s0:s1], in0=sums[c, 0][:], in1=gates[:, s0:s1], op=MULT)
 
         def scatter_on_scalar(c):
-            nc.scalar.activation(windows[0][:].indirect(entries(*CUTS[c])), y[c, 0][:], COPY)
-
-        def scatter_on_vector(c):
             s0, s1 = CUTS[c]
-            nc.vector.tensor_tensor(out=windows[1][:].indirect(entries(s0, s1)), in0=y[c, 1][:], in1=gates[:, s0:s1], op=MULT)
+            nc.scalar.activation(windows[0][:].indirect(entries(s0, s1)), y[0][:, s0:s1], COPY)
 
-        last_row = LOADS[-1][1]
-        gather_on_scalar(LAST, last_row, *CUTS[0])
-        gather_on_vector(LAST, last_row, *CUTS[1])
-        gather_on_scalar(LAST, last_row, *CUTS[2])
-        interleave(nc.vector.tensor_copy, LAST, *CUTS[0])
-        interleave(nc.vector.tensor_copy, LAST, *CUTS[1])
-        interleave(nc.scalar.copy, LAST, C, SCALAR_END)
-        quantise(LAST, *CUTS[0])
-        quantise(LAST, *CUTS[1])
-        interleave(nc.vector.tensor_copy, LAST, SCALAR_END, S)
+        def scatter_on_vector(s0, s1):
+            nc.vector.tensor_tensor(
+                out=windows[1][:].indirect(entries(s0, s1)), in0=y[1][:, s0:s1], in1=gates[:, s0:s1], op=MULT
+            )
 
         for c, b in groups[:3]:
-            multiply(c, b, range(LAST))
-        for c, b in groups[:3]:
-            multiply(c, b, [LAST])
-        multiply(*groups[3], range(PASSES))
+            multiply(c, b)
         times_gate(0)
+        last_codes[C] = keep.tile([P, C], U32, name="long_codes", tag="last_codes0", align_bytes=64)
         quantise(LAST, *CUTS[2])
-        for c, b in groups[4:]:
-            multiply(c, b, range(PASSES))
-        for c in range(len(CUTS)):
-            nc.scalar.copy(out=y[c, 1][:], in_=sums[c, 1][:])
-            scatter_on_scalar(c)
-            if c + 1 < len(CUTS):
-                times_gate(c + 1)
-            scatter_on_vector(c)
+        times_gate(1)
+        for c, b in groups[3:]:
+            multiply(c, b)
+        nc.scalar.copy(out=y[1][:, : C // 2], in_=sums[0, 1][:])
+        scatter_on_scalar(0)
+        scatter_on_scalar(1)
+        scatter_on_vector(*CUTS[0])
+        nc.vector.tensor_copy(out=y[1][:, C // 2 : C], in_=sums[1, 1][:])
+        times_gate(2)
+        scatter_on_scalar(2)
+        nc.vector.tensor_copy(out=y[1][:, C:], in_=sums[2, 1][:])
+        scatter_on_vector(C // 2, S)
         for b in range(BLOCKS):
             nc.sync.dma_start(out[b * P : (b + 1) * P, :], windows[b][:])

@@ -41,6 +41,11 @@ def tile_routed_moe_kernel(tc, xT, w_words, w_scales, gate, offs, out):
         nc.vector.memset(windows[1][:], 0.0)
         nc.scalar.activation(windows[0][:], windows[1][:], COPY)
 
+        gate_row = keep.tile([P, S], F32, name="gate_row")
+        nc.vector.memset(gate_row[:], 0.0)
+        ones = keep.tile([P, P], F32, name="ones")
+        nc.vector.memset(ones[:], 1.0)
+
         x_rows = xT.rearrange("(g p t) n -> g p t n", p=P, t=PACK)
         raw = keep.tile([P, PASSES, PACK, T], F32, name="raw", align_bytes=64)
         offsets = keep.tile([P, S // 16], U16, name="offsets")
@@ -48,6 +53,8 @@ def tile_routed_moe_kernel(tc, xT, w_words, w_scales, gate, offs, out):
             nc.sync.dma_start(raw[:, g, t0 : t0 + count], x_rows[g, :, t0 : t0 + count])
             if i == 0:
                 nc.sync.dma_start(offsets[:], offs)
+            if i == len(LOADS) - 2:
+                nc.sync.dma_start(gate_row[0:1, :], gate[0:1, :])
 
         w_codes = keep.tile([P, E, PASSES, N], U32, name="w_codes", align_bytes=64)
         for q in range(4):
@@ -55,17 +62,19 @@ def tile_routed_moe_kernel(tc, xT, w_words, w_scales, gate, offs, out):
                 w_planes[32 * q : 32 * q + 4, :, :].bitcast(I32),
                 w_scales[:, :, 4 * q : 4 * q + 4, :].rearrange("e a q n -> q (e a) n").bitcast(I32),
             )
-        gates = keep.tile([P, S], F32, name="gates")
         for e in range(E):
             nc.sync.dma_start(
                 w_codes[:, e, :, :].bitcast(I32),
                 w_words[e].rearrange("a p n r -> p a (n r)").bitcast(I32),
             )
-            if e == 0:
-                nc.sync.dma_start(gates[:], gate[0:P, :])
+
+        spread = [psum.tile([P, C], F32, name=f"spread{e}") for e in range(E)]
+        for e in range(E):
+            nc.tensor.matmul(spread[e][:], ones[:], gate_row[:, e * C : (e + 1) * C], start=True, stop=True)
 
         picked = keep.tile([P, 2 * PACK - 1, S], F32, name="picked", align_bytes=64)
         grouped = keep.tile([P, PASSES, S * PACK], BF16, name="grouped", align_bytes=64)
+        first_grouped = keep.tile([P, C // 2 * PACK], BF16, name="first_grouped", tag="first", align_bytes=64)
         x_codes = keep.tile([P, LAST, S], U32, name="x_codes", align_bytes=64)
         last_codes = {
             s0: keep.tile([P, s1 - s0], U32, name=f"last_codes{s0}", tag=f"last_codes{s0}", align_bytes=64)
@@ -82,6 +91,9 @@ def tile_routed_moe_kernel(tc, xT, w_words, w_scales, gate, offs, out):
         def gather_on_scalar(g, t, s0, s1):
             nc.scalar.activation(picked[:, FIRST_PLACE[g] + t, s0:s1], raw[:, g, t].indirect(entries(s0, s1)), COPY)
 
+        def grouped_of(g, s0, s1):
+            return first_grouped[:] if (g, s0, s1) == (LAST, *CUTS[0]) else grouped[:, g, PACK * s0 : PACK * s1]
+
         def interleave(copy, g, s0, s1):
             rows = picked[:, FIRST_PLACE[g] : FIRST_PLACE[g] + PACK, s0:s1]
             copy(
@@ -96,7 +108,7 @@ def tile_routed_moe_kernel(tc, xT, w_words, w_scales, gate, offs, out):
             nc.vector.quantize_mx(
                 out=codes_of(g, s0, s1).bitcast(FP8X4),
                 scales=x_planes[:, g, s0:s1],
-                in_=grouped[:, g, PACK * s0 : PACK * s1],
+                in_=grouped_of(g, s0, s1),
             )
 
         halves = [(e * C, (e + 1) * C) for e in range(E)]
@@ -123,20 +135,24 @@ def tile_routed_moe_kernel(tc, xT, w_words, w_scales, gate, offs, out):
             gather_on_vector(LAST, 3, *half)
         for s0, s1 in CUTS[:2]:
             nc.vector.tensor_copy(
-                out=grouped[:, LAST, PACK * s0 : PACK * s1].rearrange("p (c i t) -> p c t i", i=4, t=PACK)[:, :, 1:],
+                out=grouped_of(LAST, s0, s1).rearrange("p (c i t) -> p c t i", i=4, t=PACK)[:, :, 1:],
                 in_=picked[:, 1:PACK, s0:s1].rearrange("p t (c i) -> p c t i", i=4),
             )
         for s0, s1 in CUTS[:2]:
             nc.vector.tensor_copy(
-                out=grouped[:, LAST, PACK * s0 : PACK * s1 : PACK], in_=raw[:, LAST, 0].indirect(entries(s0, s1))
+                out=grouped_of(LAST, s0, s1)[:, ::PACK], in_=raw[:, LAST, 0].indirect(entries(s0, s1))
             )
         quantise(LAST, *CUTS[0])
         quantise(LAST, *CUTS[1])
+        gates = keep.tile([P, S], F32, name="gates", tag="first", align_bytes=64)
+        for s0, s1 in CUTS[:2]:
+            nc.vector.tensor_copy(out=gates[:, s0:s1], in_=spread[0][:, s0:s1])
         pieces = [(C, C + C // 2), (C + C // 2, S)]
         for piece in pieces:
             gather_on_scalar(LAST, 0, *piece)
         for piece in pieces:
             interleave(nc.scalar.copy, LAST, *piece)
+        nc.scalar.copy(out=gates[:, C:], in_=spread[1][:])
 
         groups = [(c, b) for c in range(len(CUTS)) for b in range(BLOCKS)]
         sums = {(c, b): psum.tile([P, CUTS[c][1] - CUTS[c][0]], F32, name=f"sums{c}_{b}") for c, b in groups}
@@ -179,14 +195,14 @@ def tile_routed_moe_kernel(tc, xT, w_words, w_scales, gate, offs, out):
         times_gate(1)
         for c, b in groups[3:]:
             multiply(c, b)
-        nc.scalar.copy(out=y[1][:, : C // 2], in_=sums[0, 1][:])
+        nc.vector.tensor_copy(out=y[1][:, : C // 2], in_=sums[0, 1][:])
         scatter_on_scalar(0)
+        nc.scalar.copy(out=y[1][:, C // 2 : C], in_=sums[1, 1][:])
         scatter_on_scalar(1)
+        nc.scalar.copy(out=y[1][:, C:], in_=sums[2, 1][:])
         scatter_on_vector(*CUTS[0])
-        nc.vector.tensor_copy(out=y[1][:, C // 2 : C], in_=sums[1, 1][:])
         times_gate(2)
         scatter_on_scalar(2)
-        nc.vector.tensor_copy(out=y[1][:, C:], in_=sums[2, 1][:])
         scatter_on_vector(C // 2, S)
         for b in range(BLOCKS):
             nc.sync.dma_start(out[b * P : (b + 1) * P, :], windows[b][:])

@@ -23,10 +23,10 @@ FP8X4 = mybir.dt.float8_e4m3fn_x4
 MULT = mybir.AluOpType.mult
 COPY = mybir.ActivationFunctionType.Copy
 
-LOADS = [(0, 0, 2), (0, 2, 2), (1, 2, 2), (1, 0, 2), (2, 1, 2), (2, 3, 1), (2, 0, 1)]
-FIRST_PLACE = [0, 3, 0]
-SHARED_PLACE = 3
+LOADS = [(0, 0, 2), (0, 2, 2), (1, 0, 2), (1, 2, 2), (2, 1, 2), (2, 3, 1), (2, 0, 1)]
+HALVES = [(e * C, (e + 1) * C) for e in range(E)]
 CUTS = [(0, C // 2), (C // 2, C), (C, S)]
+PIECES = [(C, C + C // 2), (C + C // 2, S)]
 
 
 def tile_routed_moe_kernel(tc, xT, w_words, w_scales, gate, offs, out):
@@ -40,7 +40,6 @@ def tile_routed_moe_kernel(tc, xT, w_words, w_scales, gate, offs, out):
         windows = [keep.tile([P, T], F32, name=f"window{b}") for b in range(BLOCKS)]
         nc.vector.memset(windows[1][:], 0.0)
         nc.scalar.activation(windows[0][:], windows[1][:], COPY)
-
         gate_row = keep.tile([P, S], F32, name="gate_row")
         nc.vector.memset(gate_row[:], 0.0)
         ones = keep.tile([P, P], F32, name="ones")
@@ -69,12 +68,14 @@ def tile_routed_moe_kernel(tc, xT, w_words, w_scales, gate, offs, out):
             )
 
         spread = [psum.tile([P, C], F32, name=f"spread{e}") for e in range(E)]
-        for e in range(E):
-            nc.tensor.matmul(spread[e][:], ones[:], gate_row[:, e * C : (e + 1) * C], start=True, stop=True)
+        for e, (s0, s1) in enumerate(HALVES):
+            nc.tensor.matmul(spread[e][:], ones[:], gate_row[:, s0:s1], start=True, stop=True)
 
-        picked = keep.tile([P, 2 * PACK - 1, S], F32, name="picked", align_bytes=64)
-        grouped = keep.tile([P, PASSES, S * PACK], BF16, name="grouped", align_bytes=64)
-        first_grouped = keep.tile([P, C // 2 * PACK], BF16, name="first_grouped", tag="first", align_bytes=64)
+        picked = keep.tile([P, LAST, PACK, S], F32, name="picked", align_bytes=64)
+        grouped = keep.tile([P, LAST, S * PACK], BF16, name="grouped", align_bytes=64)
+        last_picked = [keep.tile([P, PACK, C], F32, name=f"last_picked{e}", align_bytes=64) for e in range(E)]
+        gates = keep.tile([P, S], F32, name="gates", align_bytes=64)
+        inputs = {0: gates[:, :C], C // 2: gates[:, C:]}
         x_codes = keep.tile([P, LAST, S], U32, name="x_codes", align_bytes=64)
         last_codes = {
             s0: keep.tile([P, s1 - s0], U32, name=f"last_codes{s0}", tag=f"last_codes{s0}", align_bytes=64)
@@ -85,73 +86,66 @@ def tile_routed_moe_kernel(tc, xT, w_words, w_scales, gate, offs, out):
         def entries(s0, s1):
             return offsets[:, s0 // 16 : s1 // 16]
 
-        def gather_on_vector(g, t, s0, s1):
-            nc.vector.tensor_copy(out=picked[:, FIRST_PLACE[g] + t, s0:s1], in_=raw[:, g, t].indirect(entries(s0, s1)))
-
-        def gather_on_scalar(g, t, s0, s1):
-            nc.scalar.activation(picked[:, FIRST_PLACE[g] + t, s0:s1], raw[:, g, t].indirect(entries(s0, s1)), COPY)
+        def rows_of(g, s0, s1):
+            if g < LAST:
+                return picked[:, g, :, s0:s1]
+            return last_picked[s0 // C][:, :, s0 % C : s0 % C + s1 - s0]
 
         def grouped_of(g, s0, s1):
-            return first_grouped[:] if (g, s0, s1) == (LAST, *CUTS[0]) else grouped[:, g, PACK * s0 : PACK * s1]
-
-        def interleave(copy, g, s0, s1):
-            rows = picked[:, FIRST_PLACE[g] : FIRST_PLACE[g] + PACK, s0:s1]
-            copy(
-                out=grouped[:, g, PACK * s0 : PACK * s1].rearrange("p (c i t) -> p c t i", i=4, t=PACK),
-                in_=rows.rearrange("p t (c i) -> p c t i", i=4),
-            )
+            if g < LAST:
+                return grouped[:, g, PACK * s0 : PACK * s1]
+            return inputs[s0].bitcast(BF16)
 
         def codes_of(g, s0, s1):
-            return x_codes[:, g, s0:s1] if g < LAST else last_codes[s0][:]
+            if g < LAST:
+                return x_codes[:, g, s0:s1]
+            return last_codes[s0][:] if s0 < C else last_codes[C][:, s0 - C : s1 - C]
+
+        def gather_on_vector(g, t, s0, s1):
+            nc.vector.tensor_copy(out=rows_of(g, s0, s1)[:, t], in_=raw[:, g, t].indirect(entries(s0, s1)))
+
+        def gather_on_scalar(g, t, s0, s1):
+            nc.scalar.activation(rows_of(g, s0, s1)[:, t], raw[:, g, t].indirect(entries(s0, s1)), COPY)
+
+        def interleave(g, s0, s1, first_row=0):
+            nc.vector.tensor_copy(
+                out=grouped_of(g, s0, s1).rearrange("p (c i t) -> p c t i", i=4, t=PACK)[:, :, first_row:],
+                in_=rows_of(g, s0, s1)[:, first_row:].rearrange("p t (c i) -> p c t i", i=4),
+            )
 
         def quantise(g, s0, s1):
             nc.vector.quantize_mx(
-                out=codes_of(g, s0, s1).bitcast(FP8X4),
-                scales=x_planes[:, g, s0:s1],
-                in_=grouped_of(g, s0, s1),
+                out=codes_of(g, s0, s1).bitcast(FP8X4), scales=x_planes[:, g, s0:s1], in_=grouped_of(g, s0, s1)
             )
 
-        halves = [(e * C, (e + 1) * C) for e in range(E)]
-        for g, t0, count in LOADS[: 2 * LAST]:
-            closing = t0 <= SHARED_PLACE - FIRST_PLACE[g] < t0 + count
-            for t in range(t0, t0 + count):
-                if FIRST_PLACE[g] + t == SHARED_PLACE:
-                    gather_on_vector(g, t, 0, S)
-                elif closing:
-                    for half in halves:
-                        gather_on_scalar(g, t, *half)
-                else:
-                    gather_on_scalar(g, t, 0, S)
-            if closing:
-                for half in halves:
-                    interleave(nc.vector.tensor_copy, g, *half)
-                for half in halves:
-                    quantise(g, *half)
+        for g in range(LAST):
+            for t in (0, 1):
+                gather_on_scalar(g, t, 0, S)
+            for half in HALVES:
+                gather_on_scalar(g, 2, *half)
+            gather_on_vector(g, 3, 0, S)
+            for half in HALVES:
+                interleave(g, *half)
+            for half in HALVES:
+                quantise(g, *half)
 
-        for half in halves:
+        for half in HALVES:
             for t in (1, 2):
                 gather_on_scalar(LAST, t, *half)
-        for half in halves:
-            gather_on_vector(LAST, 3, *half)
+        gather_on_vector(LAST, 3, *HALVES[0])
+        gather_on_vector(LAST, 3, *PIECES[0])
+        for cut in CUTS[:2]:
+            interleave(LAST, *cut, first_row=1)
         for s0, s1 in CUTS[:2]:
-            nc.vector.tensor_copy(
-                out=grouped_of(LAST, s0, s1).rearrange("p (c i t) -> p c t i", i=4, t=PACK)[:, :, 1:],
-                in_=picked[:, 1:PACK, s0:s1].rearrange("p t (c i) -> p c t i", i=4),
-            )
-        for s0, s1 in CUTS[:2]:
-            nc.vector.tensor_copy(
-                out=grouped_of(LAST, s0, s1)[:, ::PACK], in_=raw[:, LAST, 0].indirect(entries(s0, s1))
-            )
-        quantise(LAST, *CUTS[0])
-        quantise(LAST, *CUTS[1])
-        gates = keep.tile([P, S], F32, name="gates", tag="first", align_bytes=64)
-        for s0, s1 in CUTS[:2]:
-            nc.vector.tensor_copy(out=gates[:, s0:s1], in_=spread[0][:, s0:s1])
-        pieces = [(C, C + C // 2), (C + C // 2, S)]
-        for piece in pieces:
-            gather_on_scalar(LAST, 0, *piece)
-        for piece in pieces:
-            interleave(nc.scalar.copy, LAST, *piece)
+            nc.vector.tensor_copy(out=grouped_of(LAST, s0, s1)[:, ::PACK], in_=raw[:, LAST, 0].indirect(entries(s0, s1)))
+        for cut in CUTS[:2]:
+            quantise(LAST, *cut)
+        nc.vector.tensor_copy(out=gates[:, : C // 2], in_=spread[0][:, : C // 2])
+        gather_on_scalar(LAST, 0, *HALVES[1])
+        gather_on_scalar(LAST, 3, *PIECES[1])
+        inputs[C] = keep.tile([P, C], F32, name="third_input", align_bytes=64)[:]
+        interleave(LAST, *PIECES[0])
+        nc.scalar.copy(out=gates[:, C // 2 : C], in_=spread[0][:, C // 2 :])
         nc.scalar.copy(out=gates[:, C:], in_=spread[1][:])
 
         groups = [(c, b) for c in range(len(CUTS)) for b in range(BLOCKS)]
@@ -178,6 +172,10 @@ def tile_routed_moe_kernel(tc, xT, w_words, w_scales, gate, offs, out):
             s0, s1 = CUTS[c]
             nc.vector.tensor_tensor(out=y[0][:, s0:s1], in0=sums[c, 0][:], in1=gates[:, s0:s1], op=MULT)
 
+        def empty_bank(c):
+            s0, s1 = CUTS[c]
+            nc.scalar.copy(out=y[1][:, s0:s1], in_=sums[c, 1][:])
+
         def scatter_on_scalar(c):
             s0, s1 = CUTS[c]
             nc.scalar.activation(windows[0][:].indirect(entries(s0, s1)), y[0][:, s0:s1], COPY)
@@ -187,19 +185,21 @@ def tile_routed_moe_kernel(tc, xT, w_words, w_scales, gate, offs, out):
                 out=windows[1][:].indirect(entries(s0, s1)), in0=y[1][:, s0:s1], in1=gates[:, s0:s1], op=MULT
             )
 
-        for c, b in groups[:3]:
+        for c, b in groups[:4]:
             multiply(c, b)
         times_gate(0)
-        last_codes[C] = keep.tile([P, C], U32, name="long_codes", tag="last_codes0", align_bytes=64)
-        quantise(LAST, *CUTS[2])
+        inputs[PIECES[1][0]] = keep.tile([P, C], F32, name="fourth_input", tag="last_codes0", align_bytes=64)[:]
+        interleave(LAST, *PIECES[1])
         times_gate(1)
-        for c, b in groups[3:]:
+        last_codes[C] = keep.tile([P, C], U32, name="long_codes", tag=f"last_codes{C // 2}", align_bytes=64)
+        for piece in PIECES:
+            quantise(LAST, *piece)
+        for c, b in groups[4:]:
             multiply(c, b)
-        nc.vector.tensor_copy(out=y[1][:, : C // 2], in_=sums[0, 1][:])
-        scatter_on_scalar(0)
-        nc.scalar.copy(out=y[1][:, C // 2 : C], in_=sums[1, 1][:])
-        scatter_on_scalar(1)
-        nc.scalar.copy(out=y[1][:, C:], in_=sums[2, 1][:])
+        for c in range(2):
+            empty_bank(c)
+            scatter_on_scalar(c)
+        empty_bank(2)
         scatter_on_vector(*CUTS[0])
         times_gate(2)
         scatter_on_scalar(2)

@@ -37,7 +37,7 @@ def tile_routed_moe_kernel(tc, xT, w_words, w_scales, gate, offs, out):
 
         w_planes = keep.tile([P, E * PASSES, N], U8, name="w_planes", align_bytes=64)
         nc.vector.memset(w_planes[:].rearrange("p a n -> p (a n)").bitcast(I32), 0)
-        windows = [keep.tile([P, T], F32, name=f"window{b}") for b in range(BLOCKS)]
+        windows = [keep.tile([P, T], F32, name=f"window{b}", align_bytes=256) for b in range(BLOCKS)]
         nc.vector.memset(windows[1][:], 0.0)
         nc.scalar.activation(windows[0][:], windows[1][:], COPY)
         gate_row = keep.tile([P, S], F32, name="gate_row")
@@ -46,7 +46,7 @@ def tile_routed_moe_kernel(tc, xT, w_words, w_scales, gate, offs, out):
         nc.vector.memset(ones[:], 1.0)
 
         x_rows = xT.rearrange("(g p t) n -> g p t n", p=P, t=PACK)
-        raw = keep.tile([P, PASSES, PACK, T], F32, name="raw", align_bytes=64)
+        raw = keep.tile([P, PASSES, PACK, T], F32, name="raw", align_bytes=256)
         offsets = keep.tile([P, S // 16], U16, name="offsets")
         for i, (g, t0, count) in enumerate(LOADS):
             nc.sync.dma_start(raw[:, g, t0 : t0 + count], x_rows[g, :, t0 : t0 + count])
@@ -55,7 +55,7 @@ def tile_routed_moe_kernel(tc, xT, w_words, w_scales, gate, offs, out):
             if i == len(LOADS) - 2:
                 nc.sync.dma_start(gate_row[0:1, :], gate[0:1, :])
 
-        w_codes = keep.tile([P, E, PASSES, N], U32, name="w_codes", align_bytes=64)
+        w_codes = keep.tile([P, E, PASSES, N], U32, name="w_codes", align_bytes=256)
         for q in range(4):
             nc.sync.dma_start(
                 w_planes[32 * q : 32 * q + 4, :, :].bitcast(I32),

@@ -23,10 +23,10 @@ FP8X4 = mybir.dt.float8_e4m3fn_x4
 MULT = mybir.AluOpType.mult
 COPY = mybir.ActivationFunctionType.Copy
 
-LOADS = [(0, 0, 2), (0, 2, 2), (1, 0, 2), (1, 2, 2), (2, 1, 2), (2, 3, 1), (2, 0, 1)]
 HALVES = [(e * C, (e + 1) * C) for e in range(E)]
 CUTS = [(0, C // 2), (C // 2, C), (C, S)]
-PIECES = [(C, C + C // 2), (C + C // 2, S)]
+LAST_ROWS = (2, 3, 1, 0)
+SHARE = S - C // 2
 
 
 def tile_routed_moe_kernel(tc, xT, w_words, w_scales, gate, offs, out):
@@ -35,25 +35,35 @@ def tile_routed_moe_kernel(tc, xT, w_words, w_scales, gate, offs, out):
         keep = ctx.enter_context(tc.tile_pool(name="keep", bufs=1))
         psum = ctx.enter_context(tc.psum_pool(name="psum", bufs=1))
 
+        gate_row = keep.tile([P, S], F32, name="gate_row")
+        nc.vector.memset(gate_row[:], 0.0)
+        ones = keep.tile([P, P], F32, name="ones")
+        nc.vector.memset(ones[:], 1.0)
         w_planes = keep.tile([P, E * PASSES, N], U8, name="w_planes", align_bytes=64)
         nc.vector.memset(w_planes[:].rearrange("p a n -> p (a n)").bitcast(I32), 0)
         windows = [keep.tile([P, T], F32, name=f"window{b}", align_bytes=256) for b in range(BLOCKS)]
         nc.vector.memset(windows[1][:], 0.0)
         nc.scalar.activation(windows[0][:], windows[1][:], COPY)
-        gate_row = keep.tile([P, S], F32, name="gate_row")
-        nc.vector.memset(gate_row[:], 0.0)
-        ones = keep.tile([P, P], F32, name="ones")
-        nc.vector.memset(ones[:], 1.0)
 
         x_rows = xT.rearrange("(g p t) n -> g p t n", p=P, t=PACK)
-        raw = keep.tile([P, PASSES, PACK, T], F32, name="raw", align_bytes=256)
         offsets = keep.tile([P, S // 16], U16, name="offsets")
-        for i, (g, t0, count) in enumerate(LOADS):
-            nc.sync.dma_start(raw[:, g, t0 : t0 + count], x_rows[g, :, t0 : t0 + count])
-            if i == 0:
-                nc.sync.dma_start(offsets[:], offs)
-            if i == len(LOADS) - 2:
+        window_of = {}
+        for g in range(LAST):
+            for first, second in ((1, 2), (0, 3)):
+                both = keep.tile([P, 2 * T], F32, name=f"rows{g}_{first}", align_bytes=256)
+                nc.sync.dma_start(
+                    both[:].rearrange("p (t n) -> p t n", t=2), x_rows[g, :, first : second + 1 : second - first]
+                )
+                window_of[g, first] = both[:]
+                window_of[g, second] = both[:, T:]
+                if (g, first) == (0, 1):
+                    nc.sync.dma_start(offsets[:], offs)
+        for t in LAST_ROWS:
+            if t == LAST_ROWS[2]:
                 nc.sync.dma_start(gate_row[0:1, :], gate[0:1, :])
+            row = keep.tile([P, T], F32, name=f"last_row{t}", align_bytes=256)
+            nc.sync.dma_start(row[:], x_rows[LAST, :, t])
+            window_of[LAST, t] = row[:]
 
         w_codes = keep.tile([P, E, PASSES, N], U32, name="w_codes", align_bytes=256)
         for q in range(4):
@@ -61,21 +71,18 @@ def tile_routed_moe_kernel(tc, xT, w_words, w_scales, gate, offs, out):
                 w_planes[32 * q : 32 * q + 4, :, :].bitcast(I32),
                 w_scales[:, :, 4 * q : 4 * q + 4, :].rearrange("e a q n -> q (e a) n").bitcast(I32),
             )
-        for e in range(E):
+        for e, n0, n1 in ((0, 0, P), (0, P, N), (1, 0, N)):
             nc.sync.dma_start(
-                w_codes[:, e, :, :].bitcast(I32),
-                w_words[e].rearrange("a p n r -> p a (n r)").bitcast(I32),
+                w_codes[:, e, :, n0:n1].bitcast(I32),
+                w_words[e].rearrange("a p n r -> p a (n r)").bitcast(I32)[:, :, n0:n1],
             )
 
         spread = [psum.tile([P, C], F32, name=f"spread{e}") for e in range(E)]
         for e, (s0, s1) in enumerate(HALVES):
             nc.tensor.matmul(spread[e][:], ones[:], gate_row[:, s0:s1], start=True, stop=True)
 
-        picked = keep.tile([P, LAST, PACK, S], F32, name="picked", align_bytes=64)
-        grouped = keep.tile([P, LAST, S * PACK], BF16, name="grouped", align_bytes=64)
-        last_picked = [keep.tile([P, PACK, C], F32, name=f"last_picked{e}", align_bytes=64) for e in range(E)]
-        gates = keep.tile([P, S], F32, name="gates", align_bytes=64)
-        inputs = {0: gates[:, :C], C // 2: gates[:, C:]}
+        pairs = keep.tile([P, PASSES, 2, S, 2], BF16, name="pairs", align_bytes=64)
+        grouped = keep.tile([P, PASSES, S, PACK], BF16, name="grouped", align_bytes=64)
         x_codes = keep.tile([P, LAST, S], U32, name="x_codes", align_bytes=64)
         last_codes = {
             s0: keep.tile([P, s1 - s0], U32, name=f"last_codes{s0}", tag=f"last_codes{s0}", align_bytes=64)
@@ -86,95 +93,83 @@ def tile_routed_moe_kernel(tc, xT, w_words, w_scales, gate, offs, out):
         def entries(s0, s1):
             return offsets[:, s0 // 16 : s1 // 16]
 
-        def rows_of(g, s0, s1):
-            if g < LAST:
-                return picked[:, g, :, s0:s1]
-            return last_picked[s0 // C][:, :, s0 % C : s0 % C + s1 - s0]
+        def in_pair(g, t, s0, s1):
+            return pairs[:, g, t // 2, s0:s1, t % 2]
 
-        def grouped_of(g, s0, s1):
-            if g < LAST:
-                return grouped[:, g, PACK * s0 : PACK * s1]
-            return inputs[s0].bitcast(BF16)
+        def in_place(g, t, s0, s1):
+            return grouped[:, g, s0:s1, t]
 
         def codes_of(g, s0, s1):
-            if g < LAST:
-                return x_codes[:, g, s0:s1]
-            return last_codes[s0][:] if s0 < C else last_codes[C][:, s0 - C : s1 - C]
+            return x_codes[:, g, s0:s1] if g < LAST else last_codes[s0][:]
 
-        def gather_on_vector(g, t, s0, s1):
-            nc.vector.tensor_copy(out=rows_of(g, s0, s1)[:, t], in_=raw[:, g, t].indirect(entries(s0, s1)))
+        def gather_on_vector(place, g, t, s0, s1):
+            nc.vector.tensor_copy(out=place(g, t, s0, s1), in_=window_of[g, t].indirect(entries(s0, s1)))
 
-        def gather_on_scalar(g, t, s0, s1):
-            nc.scalar.activation(rows_of(g, s0, s1)[:, t], raw[:, g, t].indirect(entries(s0, s1)), COPY)
+        def gather_on_scalar(place, g, t, s0, s1):
+            nc.scalar.activation(place(g, t, s0, s1), window_of[g, t].indirect(entries(s0, s1)), COPY)
 
-        def interleave(g, s0, s1, first_row=0):
+        def interleave(g, s0, s1, first_pair=0):
             nc.vector.tensor_copy(
-                out=grouped_of(g, s0, s1).rearrange("p (c i t) -> p c t i", i=4, t=PACK)[:, :, first_row:],
-                in_=rows_of(g, s0, s1)[:, first_row:].rearrange("p t (c i) -> p c t i", i=4),
+                out=grouped[:, g, s0:s1].bitcast(F32)[:, :, first_pair:],
+                in_=pairs[:, g, first_pair:, s0:s1].bitcast(F32).rearrange("p u s o -> p s (u o)"),
             )
 
         def quantise(g, s0, s1):
             nc.vector.quantize_mx(
-                out=codes_of(g, s0, s1).bitcast(FP8X4), scales=x_planes[:, g, s0:s1], in_=grouped_of(g, s0, s1)
+                out=codes_of(g, s0, s1).bitcast(FP8X4),
+                scales=x_planes[:, g, s0:s1],
+                in_=grouped[:, g, s0:s1].rearrange("p s t -> p (s t)"),
             )
 
         for g in range(LAST):
-            for t in (0, 1):
-                gather_on_scalar(g, t, 0, S)
-            for half in HALVES:
-                gather_on_scalar(g, 2, *half)
-            gather_on_vector(g, 3, 0, S)
+            for first, second in ((1, 2), (0, 3)):
+                gather_on_scalar(in_pair, g, first, 0, S)
+                gather_on_vector(in_pair, g, second, 0, S)
             for half in HALVES:
                 interleave(g, *half)
             for half in HALVES:
                 quantise(g, *half)
 
-        for half in HALVES:
-            for t in (1, 2):
-                gather_on_scalar(LAST, t, *half)
-        gather_on_vector(LAST, 3, *HALVES[0])
-        gather_on_vector(LAST, 3, *PIECES[0])
-        for cut in CUTS[:2]:
-            interleave(LAST, *cut, first_row=1)
-        for s0, s1 in CUTS[:2]:
-            nc.vector.tensor_copy(out=grouped_of(LAST, s0, s1)[:, ::PACK], in_=raw[:, LAST, 0].indirect(entries(s0, s1)))
+        for t in LAST_ROWS[:2]:
+            gather_on_scalar(in_pair, LAST, t, 0, SHARE)
+            gather_on_vector(in_pair, LAST, t, SHARE, S)
+        interleave(LAST, *HALVES[0], first_pair=1)
+        for t in LAST_ROWS[2:]:
+            gather_on_vector(in_place, LAST, t, *CUTS[0])
+            gather_on_scalar(in_place, LAST, t, *CUTS[1])
+            gather_on_scalar(in_pair, LAST, t, *CUTS[2])
         for cut in CUTS[:2]:
             quantise(LAST, *cut)
-        nc.vector.tensor_copy(out=gates[:, : C // 2], in_=spread[0][:, : C // 2])
-        gather_on_scalar(LAST, 0, *HALVES[1])
-        gather_on_scalar(LAST, 3, *PIECES[1])
-        inputs[C] = keep.tile([P, C], F32, name="third_input", align_bytes=64)[:]
-        interleave(LAST, *PIECES[0])
-        nc.scalar.copy(out=gates[:, C // 2 : C], in_=spread[0][:, C // 2 :])
-        nc.scalar.copy(out=gates[:, C:], in_=spread[1][:])
+        interleave(LAST, *CUTS[2])
+        gates = grouped[:, LAST, :C].rearrange("p s t -> p (s t)").bitcast(F32)
+        for s0, s1 in CUTS:
+            nc.scalar.copy(out=gates[:, s0:s1], in_=spread[s0 // C][:, s0 % C : s0 % C + s1 - s0])
 
-        groups = [(c, b) for c in range(len(CUTS)) for b in range(BLOCKS)]
-        sums = {(c, b): psum.tile([P, CUTS[c][1] - CUTS[c][0]], F32, name=f"sums{c}_{b}") for c, b in groups}
+        sums = {
+            (c, b): psum.tile([P, s1 - s0], F32, name=f"sums{c}_{b}")
+            for c, (s0, s1) in enumerate(CUTS)
+            for b in range(BLOCKS)
+        }
         y = [keep.tile([P, S], F32, name=f"y{b}") for b in range(BLOCKS)]
 
         def multiply(c, b):
             s0, s1 = CUTS[c]
             e = s0 // C
             features = slice(b * P, (b + 1) * P)
-            passes = list(range(PASSES)) if c == 0 else list(reversed(range(PASSES)))
-            for g in passes:
+            for g in range(PASSES):
                 nc.tensor.matmul_mx(
                     out=sums[c, b][:],
                     lhsT=w_codes[:, e, g, features].bitcast(FP8X4),
                     lhsT_scale=w_planes[:, e * PASSES + g, features],
                     rhs=codes_of(g, s0, s1).bitcast(FP8X4),
                     rhs_scale=x_planes[:, g, s0:s1],
-                    start=(g == passes[0]),
-                    stop=(g == passes[-1]),
+                    start=(g == 0),
+                    stop=(g == LAST),
                 )
 
         def times_gate(c):
             s0, s1 = CUTS[c]
             nc.vector.tensor_tensor(out=y[0][:, s0:s1], in0=sums[c, 0][:], in1=gates[:, s0:s1], op=MULT)
-
-        def empty_bank(c):
-            s0, s1 = CUTS[c]
-            nc.scalar.copy(out=y[1][:, s0:s1], in_=sums[c, 1][:])
 
         def scatter_on_scalar(c):
             s0, s1 = CUTS[c]
@@ -185,24 +180,24 @@ def tile_routed_moe_kernel(tc, xT, w_words, w_scales, gate, offs, out):
                 out=windows[1][:].indirect(entries(s0, s1)), in0=y[1][:, s0:s1], in1=gates[:, s0:s1], op=MULT
             )
 
-        for c, b in groups[:4]:
-            multiply(c, b)
+        for b in range(BLOCKS):
+            for c in range(2):
+                multiply(c, b)
         times_gate(0)
-        inputs[PIECES[1][0]] = keep.tile([P, C], F32, name="fourth_input", tag="last_codes0", align_bytes=64)[:]
-        interleave(LAST, *PIECES[1])
         times_gate(1)
-        last_codes[C] = keep.tile([P, C], U32, name="long_codes", tag=f"last_codes{C // 2}", align_bytes=64)
-        for piece in PIECES:
-            quantise(LAST, *piece)
-        for c, b in groups[4:]:
-            multiply(c, b)
-        for c in range(2):
-            empty_bank(c)
+        last_codes[C] = keep.tile([P, C], U32, name="long_codes", tag="last_codes0", align_bytes=64)
+        quantise(LAST, *CUTS[2])
+        for b in range(BLOCKS):
+            multiply(2, b)
+        nc.vector.tensor_copy(out=y[1][:, : C // 2], in_=sums[0, 1][:])
+        scatter_on_scalar(0)
+        for c in (1, 2):
+            s0, s1 = CUTS[c]
+            nc.scalar.copy(out=y[1][:, s0:s1], in_=sums[c, 1][:])
+            if c == 2:
+                scatter_on_vector(*CUTS[0])
+                times_gate(2)
             scatter_on_scalar(c)
-        empty_bank(2)
-        scatter_on_vector(*CUTS[0])
-        times_gate(2)
-        scatter_on_scalar(2)
         scatter_on_vector(C // 2, S)
         for b in range(BLOCKS):
             nc.sync.dma_start(out[b * P : (b + 1) * P, :], windows[b][:])

@@ -66,10 +66,10 @@ def tile_routed_moe_kernel(tc, xT, w_words, w_scales, gate, offs, out):
             window_of[LAST, t] = row[:]
 
         w_codes = keep.tile([P, E, PASSES, N], U32, name="w_codes", align_bytes=256)
-        for q in range(4):
+        for r in range(4):
             nc.sync.dma_start(
-                w_planes[32 * q : 32 * q + 4, :, :].bitcast(I32),
-                w_scales[:, :, 4 * q : 4 * q + 4, :].rearrange("e a q n -> q (e a) n").bitcast(I32),
+                w_planes[r:P:32, :, :].bitcast(I32),
+                w_scales[:, :, r::4, :].rearrange("e a q n -> q (e a) n").bitcast(I32),
             )
         for e, n0, n1 in ((0, 0, P), (0, P, N), (1, 0, N)):
             nc.sync.dma_start(
@@ -77,7 +77,7 @@ def tile_routed_moe_kernel(tc, xT, w_words, w_scales, gate, offs, out):
                 w_words[e].rearrange("a p n r -> p a (n r)").bitcast(I32)[:, :, n0:n1],
             )
 
-        spread = [psum.tile([P, C], F32, name=f"spread{e}") for e in range(E)]
+        spread = [psum.tile([P, C], F32, name=f"spread{e}", tag=f"spread{e}") for e in range(E)]
         for e, (s0, s1) in enumerate(HALVES):
             nc.tensor.matmul(spread[e][:], ones[:], gate_row[:, s0:s1], start=True, stop=True)
 
@@ -142,18 +142,15 @@ def tile_routed_moe_kernel(tc, xT, w_words, w_scales, gate, offs, out):
             quantise(LAST, *cut)
         interleave(LAST, *CUTS[2])
         gates = grouped[:, LAST, :C].rearrange("p s t -> p (s t)").bitcast(F32)
-        for s0, s1 in CUTS:
-            nc.scalar.copy(out=gates[:, s0:s1], in_=spread[s0 // C][:, s0 % C : s0 % C + s1 - s0])
+        for e, (s0, s1) in enumerate(HALVES):
+            nc.scalar.copy(out=gates[:, s0:s1], in_=spread[e][:])
 
-        sums = {
-            (c, b): psum.tile([P, s1 - s0], F32, name=f"sums{c}_{b}")
-            for c, (s0, s1) in enumerate(CUTS)
-            for b in range(BLOCKS)
-        }
+        sums = {}
         y = [keep.tile([P, S], F32, name=f"y{b}") for b in range(BLOCKS)]
 
-        def multiply(c, b):
+        def multiply(c, b, bank):
             s0, s1 = CUTS[c]
+            sums[c, b] = psum.tile([P, s1 - s0], F32, name=f"sums{c}_{b}", tag=bank)
             e = s0 // C
             features = slice(b * P, (b + 1) * P)
             for g in range(PASSES):
@@ -171,8 +168,7 @@ def tile_routed_moe_kernel(tc, xT, w_words, w_scales, gate, offs, out):
             s0, s1 = CUTS[c]
             nc.vector.tensor_tensor(out=y[0][:, s0:s1], in0=sums[c, 0][:], in1=gates[:, s0:s1], op=MULT)
 
-        def scatter_on_scalar(c):
-            s0, s1 = CUTS[c]
+        def scatter_on_scalar(s0, s1):
             nc.scalar.activation(windows[0][:].indirect(entries(s0, s1)), y[0][:, s0:s1], COPY)
 
         def scatter_on_vector(s0, s1):
@@ -180,24 +176,23 @@ def tile_routed_moe_kernel(tc, xT, w_words, w_scales, gate, offs, out):
                 out=windows[1][:].indirect(entries(s0, s1)), in0=y[1][:, s0:s1], in1=gates[:, s0:s1], op=MULT
             )
 
-        for b in range(BLOCKS):
-            for c in range(2):
-                multiply(c, b)
+        for c in range(2):
+            multiply(c, 0, f"short{c}")
+        for c in range(2):
+            multiply(c, 1, f"spread{c}")
         times_gate(0)
         times_gate(1)
-        last_codes[C] = keep.tile([P, C], U32, name="long_codes", tag="last_codes0", align_bytes=64)
-        quantise(LAST, *CUTS[2])
-        for b in range(BLOCKS):
-            multiply(2, b)
         nc.vector.tensor_copy(out=y[1][:, : C // 2], in_=sums[0, 1][:])
-        scatter_on_scalar(0)
-        for c in (1, 2):
-            s0, s1 = CUTS[c]
-            nc.scalar.copy(out=y[1][:, s0:s1], in_=sums[c, 1][:])
-            if c == 2:
-                scatter_on_vector(*CUTS[0])
-                times_gate(2)
-            scatter_on_scalar(c)
+        last_codes[C] = keep.tile([P, C], U32, name="long_codes", tag=f"last_codes{C // 2}", align_bytes=64)
+        quantise(LAST, *CUTS[2])
+        multiply(2, 0, "short1")
+        multiply(2, 1, "spread0")
+        scatter_on_scalar(*HALVES[0])
+        scatter_on_vector(*CUTS[0])
+        times_gate(2)
+        nc.vector.tensor_copy(out=y[1][:, C // 2 : C], in_=sums[1, 1][:])
+        nc.scalar.copy(out=y[1][:, C:], in_=sums[2, 1][:])
+        scatter_on_scalar(*HALVES[1])
         scatter_on_vector(C // 2, S)
         for b in range(BLOCKS):
             nc.sync.dma_start(out[b * P : (b + 1) * P, :], windows[b][:])

@@ -25,7 +25,7 @@ COPY = mybir.ActivationFunctionType.Copy
 
 HALVES = [(e * C, (e + 1) * C) for e in range(E)]
 CUTS = [(0, C // 2), (C // 2, C), (C, S)]
-LAST_ROWS = (2, 3, 1, 0)
+LOADS = [(0, (1, 2)), (0, (0, 3)), (1, (1, 2)), (1, (0,)), (1, (3,)), (2, (2,)), (2, (3,)), (2, (1,)), (2, (0,))]
 SHARE = S - C // 2
 
 
@@ -48,22 +48,18 @@ def tile_routed_moe_kernel(tc, xT, w_words, w_scales, gate, offs, out):
         x_rows = xT.rearrange("(g p t) n -> g p t n", p=P, t=PACK)
         offsets = keep.tile([P, S // 16], U16, name="offsets")
         window_of = {}
-        for g in range(LAST):
-            for first, second in ((1, 2), (0, 3)):
-                both = keep.tile([P, 2 * T], F32, name=f"rows{g}_{first}", align_bytes=256)
-                nc.sync.dma_start(
-                    both[:].rearrange("p (t n) -> p t n", t=2), x_rows[g, :, first : second + 1 : second - first]
-                )
-                window_of[g, first] = both[:]
-                window_of[g, second] = both[:, T:]
-                if (g, first) == (0, 1):
-                    nc.sync.dma_start(offsets[:], offs)
-        for t in LAST_ROWS:
-            if t == LAST_ROWS[2]:
+        for i, (g, rows) in enumerate(LOADS):
+            if i == len(LOADS) - 2:
                 nc.sync.dma_start(gate_row[0:1, :], gate[0:1, :])
-            row = keep.tile([P, T], F32, name=f"last_row{t}", align_bytes=256)
-            nc.sync.dma_start(row[:], x_rows[LAST, :, t])
-            window_of[LAST, t] = row[:]
+            tag = f"rows{i}"
+            loaded = keep.tile([P, len(rows) * T], F32, name=tag, tag=tag, align_bytes=256)
+            nc.sync.dma_start(
+                loaded[:].rearrange("p (t n) -> p t n", n=T), x_rows[g, :, rows[0] : rows[-1] + 1 : max(rows[-1] - rows[0], 1)]
+            )
+            for j, t in enumerate(rows):
+                window_of[g, t] = loaded[:, j * T :]
+            if i == 0:
+                nc.sync.dma_start(offsets[:], offs)
 
         w_codes = keep.tile([P, E, PASSES, N], U32, name="w_codes", align_bytes=256)
         for r in range(4):
@@ -83,11 +79,7 @@ def tile_routed_moe_kernel(tc, xT, w_words, w_scales, gate, offs, out):
 
         pairs = keep.tile([P, PASSES, 2, S, 2], BF16, name="pairs", align_bytes=64)
         grouped = keep.tile([P, PASSES, S, PACK], BF16, name="grouped", align_bytes=64)
-        x_codes = keep.tile([P, LAST, S], U32, name="x_codes", align_bytes=64)
-        last_codes = {
-            s0: keep.tile([P, s1 - s0], U32, name=f"last_codes{s0}", tag=f"last_codes{s0}", align_bytes=64)
-            for s0, s1 in CUTS[:2]
-        }
+        x_codes = keep.tile([P, PASSES, S], U32, name="x_codes", align_bytes=64)
         x_planes = keep.tile([P, PASSES, S], U8, name="x_planes", align_bytes=64)
 
         def entries(s0, s1):
@@ -99,24 +91,21 @@ def tile_routed_moe_kernel(tc, xT, w_words, w_scales, gate, offs, out):
         def in_place(g, t, s0, s1):
             return grouped[:, g, s0:s1, t]
 
-        def codes_of(g, s0, s1):
-            return x_codes[:, g, s0:s1] if g < LAST else last_codes[s0][:]
-
         def gather_on_vector(place, g, t, s0, s1):
             nc.vector.tensor_copy(out=place(g, t, s0, s1), in_=window_of[g, t].indirect(entries(s0, s1)))
 
         def gather_on_scalar(place, g, t, s0, s1):
             nc.scalar.activation(place(g, t, s0, s1), window_of[g, t].indirect(entries(s0, s1)), COPY)
 
-        def interleave(g, s0, s1, first_pair=0):
+        def interleave(g, s0, s1):
             nc.vector.tensor_copy(
-                out=grouped[:, g, s0:s1].bitcast(F32)[:, :, first_pair:],
-                in_=pairs[:, g, first_pair:, s0:s1].bitcast(F32).rearrange("p u s o -> p s (u o)"),
+                out=grouped[:, g, s0:s1].bitcast(F32),
+                in_=pairs[:, g, :, s0:s1].bitcast(F32).rearrange("p u s o -> p s (u o)"),
             )
 
         def quantise(g, s0, s1):
             nc.vector.quantize_mx(
-                out=codes_of(g, s0, s1).bitcast(FP8X4),
+                out=x_codes[:, g, s0:s1].bitcast(FP8X4),
                 scales=x_planes[:, g, s0:s1],
                 in_=grouped[:, g, s0:s1].rearrange("p s t -> p (s t)"),
             )
@@ -130,20 +119,24 @@ def tile_routed_moe_kernel(tc, xT, w_words, w_scales, gate, offs, out):
             for half in HALVES:
                 quantise(g, *half)
 
-        for t in LAST_ROWS[:2]:
-            gather_on_scalar(in_pair, LAST, t, 0, SHARE)
+        for t in (2, 3):
+            gather_on_scalar(in_place, LAST, t, 0, SHARE)
             gather_on_vector(in_pair, LAST, t, SHARE, S)
-        interleave(LAST, *HALVES[0], first_pair=1)
-        for t in LAST_ROWS[2:]:
-            gather_on_vector(in_place, LAST, t, *CUTS[0])
-            gather_on_scalar(in_place, LAST, t, *CUTS[1])
-            gather_on_scalar(in_pair, LAST, t, *CUTS[2])
+        gather_on_vector(in_place, LAST, 1, *CUTS[0])
+        gather_on_vector(in_pair, LAST, 1, SHARE, S)
+        gather_on_scalar(in_place, LAST, 1, C // 2, SHARE)
+        gather_on_vector(in_place, LAST, 0, *CUTS[0])
+        gather_on_vector(in_pair, LAST, 0, SHARE, S)
+        gather_on_scalar(in_place, LAST, 0, *CUTS[1])
+        gather_on_scalar(in_place, LAST, 0, C, SHARE)
+        gates = keep.tile([P, S], F32, name="gates", tag=f"rows{len(LOADS) - 1}", align_bytes=256)
+        for s0, s1 in CUTS:
+            nc.scalar.copy(out=gates[:, s0:s1], in_=spread[s0 // C][:, s0 % C : s0 % C + s1 - s0])
         for cut in CUTS[:2]:
             quantise(LAST, *cut)
-        interleave(LAST, *CUTS[2])
-        gates = grouped[:, LAST, :C].rearrange("p s t -> p (s t)").bitcast(F32)
-        for e, (s0, s1) in enumerate(HALVES):
-            nc.scalar.copy(out=gates[:, s0:s1], in_=spread[e][:])
+        interleave(LAST, SHARE, S)
+        quantise(LAST, C, SHARE)
+        quantise(LAST, SHARE, S)
 
         sums = {}
         y = [keep.tile([P, S], F32, name=f"y{b}") for b in range(BLOCKS)]
@@ -158,7 +151,7 @@ def tile_routed_moe_kernel(tc, xT, w_words, w_scales, gate, offs, out):
                     out=sums[c, b][:],
                     lhsT=w_codes[:, e, g, features].bitcast(FP8X4),
                     lhsT_scale=w_planes[:, e * PASSES + g, features],
-                    rhs=codes_of(g, s0, s1).bitcast(FP8X4),
+                    rhs=x_codes[:, g, s0:s1].bitcast(FP8X4),
                     rhs_scale=x_planes[:, g, s0:s1],
                     start=(g == 0),
                     stop=(g == LAST),
@@ -183,14 +176,12 @@ def tile_routed_moe_kernel(tc, xT, w_words, w_scales, gate, offs, out):
         times_gate(0)
         times_gate(1)
         nc.vector.tensor_copy(out=y[1][:, : C // 2], in_=sums[0, 1][:])
-        last_codes[C] = keep.tile([P, C], U32, name="long_codes", tag=f"last_codes{C // 2}", align_bytes=64)
-        quantise(LAST, *CUTS[2])
+        nc.vector.tensor_copy(out=y[1][:, C // 2 : C], in_=sums[1, 1][:])
         multiply(2, 0, "short1")
         multiply(2, 1, "spread0")
         scatter_on_scalar(*HALVES[0])
         scatter_on_vector(*CUTS[0])
         times_gate(2)
-        nc.vector.tensor_copy(out=y[1][:, C // 2 : C], in_=sums[1, 1][:])
         nc.scalar.copy(out=y[1][:, C:], in_=sums[2, 1][:])
         scatter_on_scalar(*HALVES[1])
         scatter_on_vector(C // 2, S)

@@ -25,7 +25,7 @@ COPY = mybir.ActivationFunctionType.Copy
 
 HALVES = [(e * C, (e + 1) * C) for e in range(E)]
 CUTS = [(0, C // 2), (C // 2, C), (C, S)]
-LOADS = [(0, (1, 2)), (0, (0, 3)), (1, (1, 2)), (1, (0,)), (1, (3,)), (2, (2,)), (2, (3,)), (2, (1,)), (2, (0,))]
+LOADS = [(0, (0, 1)), (0, (2, 3)), (1, (1, 2)), (1, (0, 3)), (2, (2,)), (2, (3,)), (2, (1,)), (2, (0,))]
 SHARE = S - C // 2
 
 
@@ -36,9 +36,8 @@ def tile_routed_moe_kernel(tc, xT, w_words, w_scales, gate, offs, out):
         psum = ctx.enter_context(tc.psum_pool(name="psum", bufs=1))
 
         gate_row = keep.tile([P, S], F32, name="gate_row")
-        nc.vector.memset(gate_row[:], 0.0)
-        ones = keep.tile([P, P], F32, name="ones")
-        nc.vector.memset(ones[:], 1.0)
+        nc.vector.memset(gate_row[: P - 1, :], 0.0)
+        nc.scalar.dma_start(gate_row[P - 1 :, :], gate[0:1, :])
         w_planes = keep.tile([P, E * PASSES, N], U8, name="w_planes", align_bytes=64)
         nc.vector.memset(w_planes[:].rearrange("p a n -> p (a n)").bitcast(I32), 0)
         windows = [keep.tile([P, T], F32, name=f"window{b}", align_bytes=256) for b in range(BLOCKS)]
@@ -49,15 +48,13 @@ def tile_routed_moe_kernel(tc, xT, w_words, w_scales, gate, offs, out):
         offsets = keep.tile([P, S // 16], U16, name="offsets")
         window_of = {}
         for i, (g, rows) in enumerate(LOADS):
-            if i == len(LOADS) - 2:
-                nc.sync.dma_start(gate_row[0:1, :], gate[0:1, :])
             tag = f"rows{i}"
             loaded = keep.tile([P, len(rows) * T], F32, name=tag, tag=tag, align_bytes=256)
             nc.sync.dma_start(
                 loaded[:].rearrange("p (t n) -> p t n", n=T), x_rows[g, :, rows[0] : rows[-1] + 1 : max(rows[-1] - rows[0], 1)]
             )
             for j, t in enumerate(rows):
-                window_of[g, t] = loaded[:, j * T :]
+                window_of[g, t] = loaded[:, j * T :] if g else loaded[:, j * T : (j + 1) * T]
             if i == 0:
                 nc.sync.dma_start(offsets[:], offs)
 
@@ -72,10 +69,6 @@ def tile_routed_moe_kernel(tc, xT, w_words, w_scales, gate, offs, out):
                 w_codes[:, e, :, n0:n1].bitcast(I32),
                 w_words[e].rearrange("a p n r -> p a (n r)").bitcast(I32)[:, :, n0:n1],
             )
-
-        spread = [psum.tile([P, C], F32, name=f"spread{e}", tag=f"spread{e}") for e in range(E)]
-        for e, (s0, s1) in enumerate(HALVES):
-            nc.tensor.matmul(spread[e][:], ones[:], gate_row[:, s0:s1], start=True, stop=True)
 
         pairs = keep.tile([P, PASSES, 2, S, 2], BF16, name="pairs", align_bytes=64)
         grouped = keep.tile([P, PASSES, S, PACK], BF16, name="grouped", align_bytes=64)
@@ -110,14 +103,39 @@ def tile_routed_moe_kernel(tc, xT, w_words, w_scales, gate, offs, out):
                 in_=grouped[:, g, s0:s1].rearrange("p s t -> p (s t)"),
             )
 
-        for g in range(LAST):
-            for first, second in ((1, 2), (0, 3)):
-                gather_on_scalar(in_pair, g, first, 0, S)
-                gather_on_vector(in_pair, g, second, 0, S)
-            for half in HALVES:
-                interleave(g, *half)
-            for half in HALVES:
-                quantise(g, *half)
+        picked = keep.tile([P, PACK, S], F32, name="picked", align_bytes=64)
+
+        def as_float32(g, t, s0, s1):
+            return picked[:, t, s0:s1]
+
+        gather_on_scalar(as_float32, 0, 0, 0, S)
+        gather_on_vector(as_float32, 0, 1, 0, S)
+        for half in HALVES:
+            gather_on_scalar(as_float32, 0, 2, *half)
+        gather_on_vector(as_float32, 0, 3, 0, S)
+        for s0, s1 in HALVES:
+            nc.vector.tensor_copy(
+                out=grouped[:, 0, s0:s1].rearrange("p (c i) t -> p c t i", i=4),
+                in_=picked[:, :, s0:s1].rearrange("p t (c i) -> p c t i", i=4),
+            )
+        for half in HALVES:
+            quantise(0, *half)
+
+        gather_on_scalar(in_pair, 1, 1, 0, S)
+        gather_on_vector(in_pair, 1, 2, 0, S)
+        for half in HALVES:
+            gather_on_scalar(in_pair, 1, 0, *half)
+        gather_on_vector(in_pair, 1, 3, 0, S)
+        for half in HALVES:
+            interleave(1, *half)
+        quantise(1, *HALVES[0])
+        ones = pairs[:, 1, 0, :P].bitcast(F32).rearrange("p s o -> p (s o)")
+        nc.vector.memset(ones, 1.0)
+        quantise(1, *HALVES[1])
+
+        spread = [psum.tile([P, C], F32, name=f"spread{e}", tag=f"spread{e}") for e in range(E)]
+        for e, (s0, s1) in enumerate(HALVES):
+            nc.tensor.matmul(spread[e][:], ones, gate_row[:, s0:s1], start=True, stop=True)
 
         for t in (2, 3):
             gather_on_scalar(in_place, LAST, t, 0, SHARE)

from contextlib import ExitStack

import concourse.mybir as mybir

K, T, E, C, N = 1536, 1024, 2, 256, 256
S = E * C
P = 128
PACK = 4
PASSES = K // (P * PACK)
LAST = PASSES - 1
BLOCKS = N // P

FLOPS = 2 * S * K * N
BYTES = 4 * K * T + E * K * N + E * K * N // 32 + 4 * S + 2 * 8 * 16 * (S // 16) + 4 * N * T

F32 = mybir.dt.float32
BF16 = mybir.dt.bfloat16
I32 = mybir.dt.int32
U32 = mybir.dt.uint32
U16 = mybir.dt.uint16
U8 = mybir.dt.uint8
FP8X4 = mybir.dt.float8_e4m3fn_x4
MULT = mybir.AluOpType.mult
COPY = mybir.ActivationFunctionType.Copy

HALVES = [(e * C, (e + 1) * C) for e in range(E)]
CUTS = [(0, C // 2), (C // 2, C), (C, S)]
LOADS = [(0, (0, 1)), (0, (2, 3)), (1, (1, 2)), (1, (0, 3)), (2, (2,)), (2, (3,)), (2, (1,)), (2, (0,))]
SHARE = S - C // 2


def tile_routed_moe_kernel(tc, xT, w_words, w_scales, gate, offs, out):
    nc = tc.nc
    with ExitStack() as ctx:
        keep = ctx.enter_context(tc.tile_pool(name="keep", bufs=1))
        psum = ctx.enter_context(tc.psum_pool(name="psum", bufs=1))

        gate_row = keep.tile([P, S], F32, name="gate_row")
        nc.vector.memset(gate_row[: P - 1, :], 0.0)
        nc.scalar.dma_start(gate_row[P - 1 :, :], gate[0:1, :])
        w_planes = keep.tile([P, E * PASSES, N], U8, name="w_planes", align_bytes=64)
        nc.vector.memset(w_planes[:].rearrange("p a n -> p (a n)").bitcast(I32), 0)
        windows = [keep.tile([P, T], F32, name=f"window{b}", align_bytes=256) for b in range(BLOCKS)]
        nc.vector.memset(windows[1][:], 0.0)
        nc.scalar.activation(windows[0][:], windows[1][:], COPY)

        x_rows = xT.rearrange("(g p t) n -> g p t n", p=P, t=PACK)
        offsets = keep.tile([P, S // 16], U16, name="offsets")
        window_of = {}
        for i, (g, rows) in enumerate(LOADS):
            tag = f"rows{i}"
            loaded = keep.tile([P, len(rows) * T], F32, name=tag, tag=tag, align_bytes=256)
            nc.sync.dma_start(
                loaded[:].rearrange("p (t n) -> p t n", n=T), x_rows[g, :, rows[0] : rows[-1] + 1 : max(rows[-1] - rows[0], 1)]
            )
            for j, t in enumerate(rows):
                window_of[g, t] = loaded[:, j * T :] if g else loaded[:, j * T : (j + 1) * T]
            if i == 0:
                nc.sync.dma_start(offsets[:], offs)

        w_codes = keep.tile([P, E, PASSES, N], U32, name="w_codes", align_bytes=256)
        for r in range(4):
            nc.sync.dma_start(
                w_planes[r:P:32, :, :].bitcast(I32),
                w_scales[:, :, r::4, :].rearrange("e a q n -> q (e a) n").bitcast(I32),
            )
        for e, n0, n1 in ((0, 0, P), (0, P, N), (1, 0, N)):
            nc.sync.dma_start(
                w_codes[:, e, :, n0:n1].bitcast(I32),
                w_words[e].rearrange("a p n r -> p a (n r)").bitcast(I32)[:, :, n0:n1],
            )

        pairs = keep.tile([P, PASSES, 2, S, 2], BF16, name="pairs", align_bytes=64)
        grouped = keep.tile([P, PASSES, S, PACK], BF16, name="grouped", align_bytes=64)
        x_codes = keep.tile([P, PASSES, S], U32, name="x_codes", align_bytes=64)
        x_planes = keep.tile([P, PASSES, S], U8, name="x_planes", align_bytes=64)

        def entries(s0, s1):
            return offsets[:, s0 // 16 : s1 // 16]

        def in_pair(g, t, s0, s1):
            return pairs[:, g, t // 2, s0:s1, t % 2]

        def in_place(g, t, s0, s1):
            return grouped[:, g, s0:s1, t]

        def gather_on_vector(place, g, t, s0, s1):
            nc.vector.tensor_copy(out=place(g, t, s0, s1), in_=window_of[g, t].indirect(entries(s0, s1)))

        def gather_on_scalar(place, g, t, s0, s1):
            nc.scalar.activation(place(g, t, s0, s1), window_of[g, t].indirect(entries(s0, s1)), COPY)

        def interleave(g, s0, s1):
            nc.vector.tensor_copy(
                out=grouped[:, g, s0:s1].bitcast(F32),
                in_=pairs[:, g, :, s0:s1].bitcast(F32).rearrange("p u s o -> p s (u o)"),
            )

        def quantise(g, s0, s1):
            nc.vector.quantize_mx(
                out=x_codes[:, g, s0:s1].bitcast(FP8X4),
                scales=x_planes[:, g, s0:s1],
                in_=grouped[:, g, s0:s1].rearrange("p s t -> p (s t)"),
            )

        picked = keep.tile([P, PACK, S], F32, name="picked", align_bytes=64)

        def as_float32(g, t, s0, s1):
            return picked[:, t, s0:s1]

        gather_on_scalar(as_float32, 0, 0, 0, S)
        gather_on_vector(as_float32, 0, 1, 0, S)
        for half in HALVES:
            gather_on_scalar(as_float32, 0, 2, *half)
        gather_on_vector(as_float32, 0, 3, 0, S)
        for s0, s1 in HALVES:
            nc.vector.tensor_copy(
                out=grouped[:, 0, s0:s1].rearrange("p (c i) t -> p c t i", i=4),
                in_=picked[:, :, s0:s1].rearrange("p t (c i) -> p c t i", i=4),
            )
        for half in HALVES:
            quantise(0, *half)

        gather_on_scalar(in_pair, 1, 1, 0, S)
        gather_on_vector(in_pair, 1, 2, 0, S)
        for half in HALVES:
            gather_on_scalar(in_pair, 1, 0, *half)
        gather_on_vector(in_pair, 1, 3, 0, S)
        for half in HALVES:
            interleave(1, *half)
        quantise(1, *HALVES[0])
        ones = pairs[:, 1, 0, :P].bitcast(F32).rearrange("p s o -> p (s o)")
        nc.vector.memset(ones, 1.0)
        quantise(1, *HALVES[1])

        spread = [psum.tile([P, C], F32, name=f"spread{e}", tag=f"spread{e}") for e in range(E)]
        for e, (s0, s1) in enumerate(HALVES):
            nc.tensor.matmul(spread[e][:], ones, gate_row[:, s0:s1], start=True, stop=True)

        for t in (2, 3):
            gather_on_scalar(in_place, LAST, t, 0, SHARE)
            gather_on_vector(in_pair, LAST, t, SHARE, S)
        gather_on_vector(in_place, LAST, 1, *CUTS[0])
        gather_on_vector(in_pair, LAST, 1, SHARE, S)
        gather_on_scalar(in_place, LAST, 1, C // 2, SHARE)
        gather_on_vector(in_place, LAST, 0, *CUTS[0])
        gather_on_vector(in_pair, LAST, 0, SHARE, S)
        gather_on_scalar(in_place, LAST, 0, *CUTS[1])
        gather_on_scalar(in_place, LAST, 0, C, SHARE)
        gates = keep.tile([P, S], F32, name="gates", tag=f"rows{len(LOADS) - 1}", align_bytes=256)
        for s0, s1 in CUTS:
            nc.scalar.copy(out=gates[:, s0:s1], in_=spread[s0 // C][:, s0 % C : s0 % C + s1 - s0])
        for cut in CUTS[:2]:
            quantise(LAST, *cut)
        interleave(LAST, SHARE, S)
        quantise(LAST, C, SHARE)
        quantise(LAST, SHARE, S)

        sums = {}
        y = [keep.tile([P, S], F32, name=f"y{b}") for b in range(BLOCKS)]

        def multiply(c, b, bank):
            s0, s1 = CUTS[c]
            sums[c, b] = psum.tile([P, s1 - s0], F32, name=f"sums{c}_{b}", tag=bank)
            e = s0 // C
            features = slice(b * P, (b + 1) * P)
            for g in range(PASSES):
                nc.tensor.matmul_mx(
                    out=sums[c, b][:],
                    lhsT=w_codes[:, e, g, features].bitcast(FP8X4),
                    lhsT_scale=w_planes[:, e * PASSES + g, features],
                    rhs=x_codes[:, g, s0:s1].bitcast(FP8X4),
                    rhs_scale=x_planes[:, g, s0:s1],
                    start=(g == 0),
                    stop=(g == LAST),
                )

        def times_gate(c):
            s0, s1 = CUTS[c]
            nc.vector.tensor_tensor(out=y[0][:, s0:s1], in0=sums[c, 0][:], in1=gates[:, s0:s1], op=MULT)

        def scatter_on_scalar(s0, s1):
            nc.scalar.activation(windows[0][:].indirect(entries(s0, s1)), y[0][:, s0:s1], COPY)

        def scatter_on_vector(s0, s1):
            nc.vector.tensor_tensor(
                out=windows[1][:].indirect(entries(s0, s1)), in0=y[1][:, s0:s1], in1=gates[:, s0:s1], op=MULT
            )

        for c in range(2):
            multiply(c, 0, f"short{c}")
        for c in range(2):
            multiply(c, 1, f"spread{c}")
        times_gate(0)
        times_gate(1)
        nc.vector.tensor_copy(out=y[1][:, : C // 2], in_=sums[0, 1][:])
        nc.vector.tensor_copy(out=y[1][:, C // 2 : C], in_=sums[1, 1][:])
        multiply(2, 0, "short1")
        multiply(2, 1, "spread0")
        scatter_on_scalar(*HALVES[0])
        scatter_on_vector(*CUTS[0])
        times_gate(2)
        nc.scalar.copy(out=y[1][:, C:], in_=sums[2, 1][:])
        scatter_on_scalar(*HALVES[1])
        scatter_on_vector(C // 2, S)
        for b in range(BLOCKS):
            nc.sync.dma_start(out[b * P : (b + 1) * P, :], windows[b][:])
